import numpy as np
import ml_dtypes


def mxq(x, axis, fmt="e4m3"):
    dtype, down = {"e4m3": (ml_dtypes.float8_e4m3fn, 7), "e5m2": (ml_dtypes.float8_e5m2, 14)}[fmt]
    v = np.moveaxis(np.asarray(x, np.float32).astype(ml_dtypes.bfloat16).astype(np.float64), axis, -1)
    blocks = v.reshape(v.shape[:-1] + (-1, 32))
    amax = np.abs(blocks).max(-1, keepdims=True)
    byte = np.maximum(np.where(amax > 0, np.frexp(amax)[1] - 1 + 127, 0) - down, 1)
    scale = np.exp2(byte - 127.0)
    codes = (blocks / scale).astype(np.float32).astype(dtype).astype(np.float64)
    return np.moveaxis((codes * scale).reshape(v.shape), -1, axis)


WIDE = False


def mx_kscale(k):
    if not WIDE:
        return np.ones(k)
    levels = np.array([10, -10, 5, -5, 0])
    if k % 512:
        return np.exp2(np.random.permutation(np.resize(levels, k // 32))).repeat(32)
    a = np.empty((k // 512, 16))
    for p in range(k // 512):
        a[p, :8] = np.random.permutation(np.resize(levels, 8))
        for g in range(8):
            far = levels[np.abs(levels - a[p, g]) >= 10]
            a[p, g + 8] = far[np.random.randint(len(far))]
    return np.exp2(a.ravel()).repeat(32)


def f64(x):
    return np.asarray(x).astype(np.float64)


def striped(idx):
    return np.tile(idx.reshape(-1, 16).T, (8, 1)).astype(np.uint16)


def unstriped(offs):
    return offs[:16].T.reshape(-1).astype(np.int64)


def pack_weight(w):
    k, n = w.shape
    w = f64(np.asarray(w, np.float32).astype(ml_dtypes.bfloat16)).reshape(k // 32, 32, n)
    amax = np.abs(w).max(1)
    byte = np.clip(np.where(amax > 0, np.frexp(amax)[1] - 1 + 127 - 7, 1), 1, 254)
    scaled = (w * np.exp2(127.0 - byte)[:, None, :]).reshape(k, n).astype(np.float32)
    words = np.ascontiguousarray(scaled.reshape(k // 512, 128, 4, n).transpose(0, 1, 3, 2)).astype(ml_dtypes.float8_e4m3fn).view(np.uint8)
    return words, np.ascontiguousarray(byte.astype(np.uint8).reshape(k // 512, 16, n))


def unpack_weight(words, scales):
    g, p, n, _ = words.shape
    vals = np.ascontiguousarray(words).view(ml_dtypes.float8_e4m3fn).astype(np.float64) * np.repeat(np.exp2(scales.astype(np.float64) - 127.0), 8, axis=1)[..., None]
    return vals.transpose(0, 1, 3, 2).reshape(g * 512, n)


def sigmoid(v):
    return 1.0 / (1.0 + np.exp(-np.maximum(v, -700.0)))


K, T, S, N, U = 1024, 2048, 1024, 128, 1024


def setup_inputs():
    n = np.random.standard_normal
    s = mx_kscale(K)[:, None]
    packed_xT = pack_weight(n((K, T)) * s)
    return {
        "x_words": packed_xT[0],
        "x_scales": packed_xT[1],
        "w1": (n((K, N)) / np.sqrt(K) / s).astype(np.float32),
        "w2": (n((K, N)) / np.sqrt(K) / s).astype(np.float32),
        "w3": (n((K, N)) / np.sqrt(K) / s).astype(np.float32),
        "offs": striped(np.random.permutation(T)[:S]),
        "src": striped(np.random.permutation(S)[(S * np.random.uniform(0, 1, U) ** 4).astype(np.int64)]),
        "dst": striped(np.random.permutation(S)),
    }


def reference(x_words, x_scales, w1, w2, w3, offs, src, dst):
    xq = unpack_weight(x_words, x_scales)[:, unstriped(offs)]
    y = mxq(f64(w1), 0, "e4m3").T @ xq
    e = mxq(f64(w2), 0, "e4m3").T @ xq
    h = mxq(f64(w3), 0, "e4m3").T @ xq
    return (sigmoid(y[:, unstriped(dst)] + e[:, unstriped(src)])) * h[:, unstriped(src)]

@@ -1,0 +1,158 @@
+from contextlib import ExitStack
+
+import concourse.mybir as mybir
+
+K, T, S, M, U = 1024, 2048, 1024, 128, 1024
+FLOPS = 3 * 2 * K * M * S
+
+F32 = mybir.dt.float32
+BF16 = mybir.dt.bfloat16
+I32 = mybir.dt.int32
+U32 = mybir.dt.uint32
+U16 = mybir.dt.uint16
+U8 = mybir.dt.uint8
+FP8X4 = mybir.dt.float8_e4m3fn_x4
+ADD = mybir.AluOpType.add
+MULT = mybir.AluOpType.mult
+SIGMOID = mybir.ActivationFunctionType.Sigmoid
+
+P = 128
+PACK = 4
+K_PASS = P * PACK
+PASSES = K // K_PASS
+GROUP = 16
+
+
+def tile_picked_edgeatt_sigmoid_p_kernel(tc, x_words, x_scales, w1, w2, w3, offs, src, dst, out):
+    nc = tc.nc
+    with ExitStack() as ctx:
+        keep = ctx.enter_context(tc.tile_pool(name="keep", bufs=1))
+        psum = ctx.enter_context(tc.psum_pool(name="psum", bufs=1))
+
+        def entries(list_tile, lo, hi):
+            return list_tile[:, lo // GROUP : hi // GROUP]
+
+        offs_sb = keep.tile([P, S // GROUP], U16, name="offs_sb")
+        dst_sb = keep.tile([P, U // GROUP], U16, name="dst_sb")
+        src_sb = keep.tile([P, U // GROUP], U16, name="src_sb")
+        scale_table = keep.tile([P, T], U8, name="scale_table", align_bytes=64)
+        nc.vector.memset(scale_table[:].bitcast(I32), 0)
+        warm_in = keep.tile([P, 1], F32, name="warm_in")
+        warm_out = keep.tile([P, 1], F32, name="warm_out")
+        nc.gpsimd.memset(warm_in[:], 0.0)
+        nc.scalar.activation(warm_out[:], warm_in[:], SIGMOID)
+
+        nc.sync.dma_start(offs_sb[:], offs)
+        nc.sync.dma_start(dst_sb[:], dst)
+        nc.sync.dma_start(src_sb[:], src)
+        for q in range(4):
+            nc.sync.dma_start(
+                scale_table[32 * q : 32 * q + 8, :].bitcast(I32),
+                x_scales[:, 4 * q : 4 * q + 4, :].bitcast(I32),
+            )
+
+        def load_words(z):
+            table = keep.tile([P, T], U32, name=f"word_table{z}", align_bytes=64)
+            nc.sync.dma_start(table[:].bitcast(I32), x_words[z].rearrange("p n t -> p (n t)").bitcast(I32))
+            return table
+
+        def load_weight(w, name, z0, z1):
+            raw = keep.tile([P, z1 - z0, PACK, M], F32, name=name + "_raw")
+            nc.sync.dma_start(
+                raw[:].rearrange("p z j m -> p z (j m)"),
+                w[z0 * K_PASS : z1 * K_PASS, :].rearrange("(z p j) m -> p z (j m)", p=P, j=PACK),
+            )
+            return raw
+
+        def interleave(raw, name):
+            nz = raw.shape[1]
+            grouped = keep.tile([P, nz, M, PACK], BF16, name=name + "_bf16", align_bytes=64)
+            nc.scalar.copy(
+                grouped[:].rearrange("p z (c i) j -> p z c j i", i=4),
+                raw[:].rearrange("p z j (c i) -> p z c j i", i=4),
+            )
+            return grouped
+
+        def quantize(grouped, name):
+            nz = grouped.shape[1]
+            codes = keep.tile([P, nz * M], U32, name=name + "_codes", align_bytes=64)
+            scales = keep.tile([P, nz * M], U8, name=name + "_scales", align_bytes=64)
+            nc.vector.quantize_mx(
+                out=codes[:].bitcast(FP8X4), scales=scales[:], in_=grouped[:].rearrange("p z m j -> p (z m j)")
+            )
+            return [(codes[:, i * M : (i + 1) * M], scales[:, i * M : (i + 1) * M]) for i in range(nz)]
+
+        table0 = load_words(0)
+        w1a_raw = load_weight(w1, "w1a", 0, 1)
+        table1 = load_words(1)
+        w1b_raw = load_weight(w1, "w1b", 1, 2)
+        w2_raw = load_weight(w2, "w2", 0, 2)
+        w3_raw = load_weight(w3, "w3", 0, 2)
+
+        x_sc = keep.tile([P, S], U8, name="x_sc", align_bytes=64)
+        x0 = keep.tile([P, S], U32, name="x0", align_bytes=64)
+        x1 = keep.tile([P, S], U32, name="x1", align_bytes=64)
+        xs = [x0, x1]
+
+        def product(bank, wq, z, lo, hi):
+            codes, scales = wq[z]
+            nc.tensor.matmul_mx(
+                out=bank[:],
+                lhsT=codes.bitcast(FP8X4),
+                lhsT_scale=scales,
+                rhs=xs[z][:, lo:hi].bitcast(FP8X4),
+                rhs_scale=x_sc[4 * z : P, lo:hi],
+                start=(z == 0),
+                stop=(z == PASSES - 1),
+            )
+
+        nc.vector.tensor_copy(x_sc[:], scale_table[:].indirect(offs_sb[:]))
+        nc.vector.tensor_copy(x0[:], table0[:].indirect(offs_sb[:]))
+        w1q = quantize(interleave(w1a_raw, "w1a"), "w1a")
+
+        y_parts = [(0, 512), (512, 768), (768, 1024)]
+        halves = [(0, 512), (512, 1024)]
+        y_banks = [psum.tile([P, hi - lo], F32, name=f"y_bank{lo}") for lo, hi in y_parts]
+        e_banks = [psum.tile([P, hi - lo], F32, name=f"e_bank{lo}") for lo, hi in halves]
+        h_banks = [psum.tile([P, hi - lo], F32, name=f"h_bank{lo}") for lo, hi in halves]
+        y = keep.tile([P, S], F32, name="y")
+        e = keep.tile([P, S], F32, name="e")
+        h = keep.tile([P, S], F32, name="h")
+
+        for bank, (lo, hi) in zip(y_banks, y_parts):
+            product(bank, w1q, 0, lo, hi)
+
+        w1b_bf = interleave(w1b_raw, "w1b")
+        w2_bf = interleave(w2_raw, "w2")
+        for i, (bank, (lo, hi)) in enumerate(zip(y_banks, y_parts)):
+            nc.vector.tensor_copy(x1[:, lo:hi], table1[:].indirect(entries(offs_sb, lo, hi)))
+            if i == 0:
+                w1q = w1q + quantize(w1b_bf, "w1b")
+            product(bank, w1q, 1, lo, hi)
+            nc.scalar.copy(y[:, lo:hi], bank[:])
+
+        w2q = quantize(w2_bf, "w2")
+        w3_bf = interleave(w3_raw, "w3")
+        for bank, (lo, hi) in zip(e_banks, halves):
+            for z in range(PASSES):
+                product(bank, w2q, z, lo, hi)
+            nc.scalar.copy(e[:, lo:hi], bank[:])
+
+        y_dst = keep.tile([P, U], F32, name="y_dst")
+        logit = keep.tile([P, U], F32, name="logit")
+        gate = keep.tile([P, U], F32, name="gate")
+        result = keep.tile([P, U], F32, name="result")
+        nc.vector.tensor_copy(y_dst[:, 0:512], y[:].indirect(entries(dst_sb, 0, 512)))
+        w3q = quantize(w3_bf, "w3")
+        nc.vector.tensor_copy(y_dst[:, 512:1024], y[:].indirect(entries(dst_sb, 512, 1024)))
+        for bank, (lo, hi) in zip(h_banks, halves):
+            for z in range(PASSES):
+                product(bank, w3q, z, lo, hi)
+            nc.scalar.copy(h[:, lo:hi], bank[:])
+
+        for lo, hi in halves:
+            nc.vector.tensor_tensor(logit[:, lo:hi], e[:].indirect(entries(src_sb, lo, hi)), y_dst[:, lo:hi], ADD)
+            nc.scalar.activation(gate[:, lo:hi], logit[:, lo:hi], SIGMOID)
+        for lo, hi in y_parts:
+            nc.vector.tensor_tensor(result[:, lo:hi], h[:].indirect(entries(src_sb, lo, hi)), gate[:, lo:hi], MULT)
+            nc.sync.dma_start(out[:, lo:hi], result[:, lo:hi])

@@ -36,63 +36,65 @@ def tile_picked_edgeatt_sigmoid_p_kernel(tc, x_words, x_scales, w1, w2, w3, offs
         dst_sb = keep.tile([P, U // GROUP], U16, name="dst_sb")
         src_sb = keep.tile([P, U // GROUP], U16, name="src_sb")
         scale_table = keep.tile([P, T], U8, name="scale_table", align_bytes=64)
-        nc.vector.memset(scale_table[:].bitcast(I32), 0)
+        nc.vector.memset(scale_table[32:64, :].bitcast(I32), 0)
+        nc.vector.memset(scale_table[64:128, :].bitcast(I32), 0)
+        x_sc = keep.tile([P, PASSES, S], U8, name="x_sc", align_bytes=64)
+        nc.vector.memset(x_sc[:].rearrange("p z s -> p (z s)").bitcast(I32), 0)
         warm_in = keep.tile([P, 1], F32, name="warm_in")
         warm_out = keep.tile([P, 1], F32, name="warm_out")
         nc.gpsimd.memset(warm_in[:], 0.0)
         nc.scalar.activation(warm_out[:], warm_in[:], SIGMOID)
 
-        nc.sync.dma_start(offs_sb[:], offs)
-        nc.sync.dma_start(dst_sb[:], dst)
-        nc.sync.dma_start(src_sb[:], src)
-        for q in range(4):
-            nc.sync.dma_start(
-                scale_table[32 * q : 32 * q + 8, :].bitcast(I32),
-                x_scales[:, 4 * q : 4 * q + 4, :].bitcast(I32),
-            )
+        def load_scales():
+            nc.sync.dma_start(scale_table[0:32, :].bitcast(I32), x_scales.rearrange("z r c -> r z c").bitcast(I32))
+
+        def place_scales(picked):
+            for q in range(4):
+                nc.scalar.dma_start(
+                    x_sc[32 * q : 32 * q + 4].rearrange("p z s -> p (z s)").bitcast(I32),
+                    picked[8 * q : 8 * q + 8, :].bitcast(I32),
+                )
 
         def load_words(z):
             table = keep.tile([P, T], U32, name=f"word_table{z}", align_bytes=64)
             nc.sync.dma_start(table[:].bitcast(I32), x_words[z].rearrange("p n t -> p (n t)").bitcast(I32))
             return table
 
-        def load_weight(w, name, z0, z1):
-            raw = keep.tile([P, z1 - z0, PACK, M], F32, name=name + "_raw")
+        def load_weight(w, name, z0, z1, tag=None):
+            raw = keep.tile([P, z1 - z0, PACK, M], F32, name=name + "_raw", tag=tag or name + "_raw", align_bytes=64)
             nc.sync.dma_start(
                 raw[:].rearrange("p z j m -> p z (j m)"),
                 w[z0 * K_PASS : z1 * K_PASS, :].rearrange("(z p j) m -> p z (j m)", p=P, j=PACK),
             )
             return raw
 
-        def interleave(raw, name):
-            nz = raw.shape[1]
-            grouped = keep.tile([P, nz, M, PACK], BF16, name=name + "_bf16", align_bytes=64)
+        def interleave(raw, grouped):
             nc.scalar.copy(
-                grouped[:].rearrange("p z (c i) j -> p z c j i", i=4),
+                grouped.rearrange("p z (c i) j -> p z c j i", i=4),
                 raw[:].rearrange("p z j (c i) -> p z c j i", i=4),
             )
-            return grouped
 
-        def quantize(grouped, name):
+        def staged(name, nz=PASSES, tag=None):
+            return keep.tile([P, nz, M, PACK], BF16, name=name + "_bf16", tag=tag or name + "_bf16", align_bytes=64)
+
+        def quantize(grouped, name, tag=None):
             nz = grouped.shape[1]
-            codes = keep.tile([P, nz * M], U32, name=name + "_codes", align_bytes=64)
+            codes = keep.tile([P, nz * M], U32, name=name + "_codes", tag=tag or name + "_codes", align_bytes=64)
             scales = keep.tile([P, nz * M], U8, name=name + "_scales", align_bytes=64)
             nc.vector.quantize_mx(
-                out=codes[:].bitcast(FP8X4), scales=scales[:], in_=grouped[:].rearrange("p z m j -> p (z m j)")
+                out=codes[:].bitcast(FP8X4), scales=scales[:], in_=grouped.rearrange("p z m j -> p (z m j)")
             )
             return [(codes[:, i * M : (i + 1) * M], scales[:, i * M : (i + 1) * M]) for i in range(nz)]
 
-        table0 = load_words(0)
-        w1a_raw = load_weight(w1, "w1a", 0, 1)
-        table1 = load_words(1)
-        w1b_raw = load_weight(w1, "w1b", 1, 2)
-        w2_raw = load_weight(w2, "w2", 0, 2)
-        w3_raw = load_weight(w3, "w3", 0, 2)
-
-        x_sc = keep.tile([P, S], U8, name="x_sc", align_bytes=64)
+        sc_picked = keep.tile([P, S], U8, name="sc_picked", align_bytes=64)
         x0 = keep.tile([P, S], U32, name="x0", align_bytes=64)
-        x1 = keep.tile([P, S], U32, name="x1", align_bytes=64)
-        xs = [x0, x1]
+        x_cols = {}
+
+        def picked_words(z, lo, hi):
+            if z == 0:
+                return x0[:, lo:hi]
+            base = lo // 512 * 512
+            return x_cols[base][:, lo - base : hi - base]
 
         def product(bank, wq, z, lo, hi):
             codes, scales = wq[z]
@@ -100,59 +102,87 @@ def tile_picked_edgeatt_sigmoid_p_kernel(tc, x_words, x_scales, w1, w2, w3, offs
                 out=bank[:],
                 lhsT=codes.bitcast(FP8X4),
                 lhsT_scale=scales,
-                rhs=xs[z][:, lo:hi].bitcast(FP8X4),
-                rhs_scale=x_sc[4 * z : P, lo:hi],
+                rhs=picked_words(z, lo, hi).bitcast(FP8X4),
+                rhs_scale=x_sc[:, z, lo:hi],
                 start=(z == 0),
                 stop=(z == PASSES - 1),
             )
 
-        nc.vector.tensor_copy(x_sc[:], scale_table[:].indirect(offs_sb[:]))
+        def probe(ap, name):
+            t = keep.tile([P, 1], ap.dtype, name=name)
+            nc.gpsimd.tensor_copy(t[:], ap)
+
+        nc.sync.dma_start(offs_sb[:], offs)
+        load_scales()
+        table0 = load_words(0)
+        w1a_raw = load_weight(w1, "w1a", 0, 1)
+        table1 = load_words(1)
+        w1b_raw = load_weight(w1, "w1b", 1, 2, tag="slot_b")
+        w2_raw = load_weight(w2, "w2", 0, 2, tag="slot_a")
+        w3_raw = load_weight(w3, "w3", 0, 2, tag="slot_c")
+        nc.sync.dma_start(dst_sb[:], dst)
+        nc.sync.dma_start(src_sb[:], src)
+
+        nc.vector.tensor_copy(sc_picked[:], scale_table[:].indirect(offs_sb[:]))
+        place_scales(sc_picked)
         nc.vector.tensor_copy(x0[:], table0[:].indirect(offs_sb[:]))
-        w1q = quantize(interleave(w1a_raw, "w1a"), "w1a")
+        w1a_bf = staged("w1a", 1)
+        interleave(w1a_raw, w1a_bf[:])
+        w1q = quantize(w1a_bf[:], "w1a")
 
         y_parts = [(0, 512), (512, 768), (768, 1024)]
         halves = [(0, 512), (512, 1024)]
+        out_parts = [(0, 512), (512, 768), (768, 896), (896, 1024)]
         y_banks = [psum.tile([P, hi - lo], F32, name=f"y_bank{lo}") for lo, hi in y_parts]
         e_banks = [psum.tile([P, hi - lo], F32, name=f"e_bank{lo}") for lo, hi in halves]
         h_banks = [psum.tile([P, hi - lo], F32, name=f"h_bank{lo}") for lo, hi in halves]
-        y = keep.tile([P, S], F32, name="y")
-        e = keep.tile([P, S], F32, name="e")
-        h = keep.tile([P, S], F32, name="h")
 
         for bank, (lo, hi) in zip(y_banks, y_parts):
             product(bank, w1q, 0, lo, hi)
 
-        w1b_bf = interleave(w1b_raw, "w1b")
-        w2_bf = interleave(w2_raw, "w2")
-        for i, (bank, (lo, hi)) in enumerate(zip(y_banks, y_parts)):
-            nc.vector.tensor_copy(x1[:, lo:hi], table1[:].indirect(entries(offs_sb, lo, hi)))
-            if i == 0:
-                w1q = w1q + quantize(w1b_bf, "w1b")
+        w1b_bf = staged("w1b", 1)
+        interleave(w1b_raw, w1b_bf[:])
+        x_cols[0] = keep.tile([P, 512], U32, name="x1_lo", align_bytes=64)
+        nc.vector.tensor_copy(x_cols[0][:], table1[:].indirect(entries(offs_sb, 0, 512)))
+        w1q = w1q + quantize(w1b_bf[:], "w1b", tag="slot_d")
+        x_cols[512] = keep.tile([P, 512], U32, name="x1_hi", tag="slot_b", align_bytes=64)
+        for lo, hi in y_parts[1:]:
+            nc.vector.tensor_copy(picked_words(1, lo, hi), table1[:].indirect(entries(offs_sb, lo, hi)))
+        for bank, (lo, hi) in zip(y_banks, y_parts):
             product(bank, w1q, 1, lo, hi)
-            nc.scalar.copy(y[:, lo:hi], bank[:])
+        w2_bf = staged("w2")
+        interleave(w2_raw, w2_bf[:])
+        w2q = quantize(w2_bf[:], "w2")
+        y = keep.tile([P, S], F32, name="y", tag="slot_a", align_bytes=64)
+        e = keep.tile([P, S], F32, name="e")
+        h = keep.tile([P, S], F32, name="h")
+        nc.scalar.copy(y[:, 0:512], y_banks[0][:])
+        nc.vector.tensor_copy(y[:, 512:768], y_banks[1][:])
+        nc.vector.tensor_copy(y[:, 768:1024], y_banks[2][:])
 
-        w2q = quantize(w2_bf, "w2")
-        w3_bf = interleave(w3_raw, "w3")
+        w3_bf = staged("w3", tag="slot_d")
+        interleave(w3_raw, w3_bf[:])
         for bank, (lo, hi) in zip(e_banks, halves):
             for z in range(PASSES):
                 product(bank, w2q, z, lo, hi)
             nc.scalar.copy(e[:, lo:hi], bank[:])
 
-        y_dst = keep.tile([P, U], F32, name="y_dst")
+        y_dst0 = keep.tile([P, 512], F32, name="y_dst0", align_bytes=64)
         logit = keep.tile([P, U], F32, name="logit")
         gate = keep.tile([P, U], F32, name="gate")
         result = keep.tile([P, U], F32, name="result")
-        nc.vector.tensor_copy(y_dst[:, 0:512], y[:].indirect(entries(dst_sb, 0, 512)))
-        w3q = quantize(w3_bf, "w3")
-        nc.vector.tensor_copy(y_dst[:, 512:1024], y[:].indirect(entries(dst_sb, 512, 1024)))
+        nc.vector.tensor_copy(y_dst0[:], y[:].indirect(entries(dst_sb, 0, 512)))
+        w3q = quantize(w3_bf[:], "w3")
+        y_dst1 = keep.tile([P, 512], F32, name="y_dst1", tag="slot_c", align_bytes=64)
+        nc.vector.tensor_copy(y_dst1[:], y[:].indirect(entries(dst_sb, 512, 1024)))
         for bank, (lo, hi) in zip(h_banks, halves):
             for z in range(PASSES):
                 product(bank, w3q, z, lo, hi)
             nc.scalar.copy(h[:, lo:hi], bank[:])
 
-        for lo, hi in halves:
-            nc.vector.tensor_tensor(logit[:, lo:hi], e[:].indirect(entries(src_sb, lo, hi)), y_dst[:, lo:hi], ADD)
+        for y_dst, (lo, hi) in zip((y_dst0, y_dst1), halves):
+            nc.vector.tensor_tensor(logit[:, lo:hi], e[:].indirect(entries(src_sb, lo, hi)), y_dst[:], ADD)
             nc.scalar.activation(gate[:, lo:hi], logit[:, lo:hi], SIGMOID)
-        for lo, hi in y_parts:
+        for lo, hi in out_parts:
             nc.vector.tensor_tensor(result[:, lo:hi], h[:].indirect(entries(src_sb, lo, hi)), gate[:, lo:hi], MULT)
             nc.sync.dma_start(out[:, lo:hi], result[:, lo:hi])

@@ -46,11 +46,11 @@ def tile_picked_edgeatt_sigmoid_p_kernel(tc, x_words, x_scales, w1, w2, w3, offs
         nc.scalar.activation(warm_out[:], warm_in[:], SIGMOID)
 
         def load_scales():
-            nc.sync.dma_start(scale_table[0:32, :].bitcast(I32), x_scales.rearrange("z r c -> r z c").bitcast(I32))
+            nc.scalar.dma_start(scale_table[0:32, :].bitcast(I32), x_scales.rearrange("z r c -> r z c").bitcast(I32))
 
         def place_scales(picked):
-            for q in range(4):
-                nc.scalar.dma_start(
+            for q in (0, 2, 1, 3):
+                nc.sync.dma_start(
                     x_sc[32 * q : 32 * q + 4].rearrange("p z s -> p (z s)").bitcast(I32),
                     picked[8 * q : 8 * q + 8, :].bitcast(I32),
                 )
@@ -93,13 +93,13 @@ def tile_picked_edgeatt_sigmoid_p_kernel(tc, x_words, x_scales, w1, w2, w3, offs
         def picked_words(z, lo, hi):
             if z == 0:
                 return x0[:, lo:hi]
-            base = lo // 512 * 512
+            base = lo // 768 * 768
             return x_cols[base][:, lo - base : hi - base]
 
         def product(bank, wq, z, lo, hi):
             codes, scales = wq[z]
             nc.tensor.matmul_mx(
-                out=bank[:],
+                out=bank,
                 lhsT=codes.bitcast(FP8X4),
                 lhsT_scale=scales,
                 rhs=picked_words(z, lo, hi).bitcast(FP8X4),
@@ -116,56 +116,62 @@ def tile_picked_edgeatt_sigmoid_p_kernel(tc, x_words, x_scales, w1, w2, w3, offs
         load_scales()
         table0 = load_words(0)
         w1a_raw = load_weight(w1, "w1a", 0, 1)
-        table1 = load_words(1)
-        w1b_raw = load_weight(w1, "w1b", 1, 2, tag="slot_b")
-        w2_raw = load_weight(w2, "w2", 0, 2, tag="slot_a")
-        w3_raw = load_weight(w3, "w3", 0, 2, tag="slot_c")
         nc.sync.dma_start(dst_sb[:], dst)
         nc.sync.dma_start(src_sb[:], src)
-
+        table1 = load_words(1)
+        w1b_raw = load_weight(w1, "w1b", 1, 2, tag="slot_b")
         nc.vector.tensor_copy(sc_picked[:], scale_table[:].indirect(offs_sb[:]))
         place_scales(sc_picked)
+        w2a_raw = load_weight(w2, "w2a", 0, 1)
+        w2b_raw = load_weight(w2, "w2b", 1, 2, tag="slot_a")
+        w3_raw = load_weight(w3, "w3", 0, 2, tag="slot_c")
         nc.vector.tensor_copy(x0[:], table0[:].indirect(offs_sb[:]))
         w1a_bf = staged("w1a", 1)
         interleave(w1a_raw, w1a_bf[:])
         w1q = quantize(w1a_bf[:], "w1a")
 
-        y_parts = [(0, 512), (512, 768), (768, 1024)]
+        y_parts = [(0, 256), (256, 512), (512, 768), (768, 896), (896, 1024)]
         halves = [(0, 512), (512, 1024)]
+        groups = [[(0, 512)], [(512, 768), (768, 1024)]]
         out_parts = [(0, 512), (512, 768), (768, 896), (896, 1024)]
-        y_banks = [psum.tile([P, hi - lo], F32, name=f"y_bank{lo}") for lo, hi in y_parts]
-        e_banks = [psum.tile([P, hi - lo], F32, name=f"e_bank{lo}") for lo, hi in halves]
-        h_banks = [psum.tile([P, hi - lo], F32, name=f"h_bank{lo}") for lo, hi in halves]
+        y_banks = [psum.tile([P, hi - lo], F32, name=f"y_bank{lo}", tag=f"bank{i}") for i, (lo, hi) in enumerate(y_parts)]
 
         for bank, (lo, hi) in zip(y_banks, y_parts):
-            product(bank, w1q, 0, lo, hi)
+            product(bank[:], w1q, 0, lo, hi)
 
         w1b_bf = staged("w1b", 1)
         interleave(w1b_raw, w1b_bf[:])
-        x_cols[0] = keep.tile([P, 512], U32, name="x1_lo", align_bytes=64)
-        nc.vector.tensor_copy(x_cols[0][:], table1[:].indirect(entries(offs_sb, 0, 512)))
-        w1q = w1q + quantize(w1b_bf[:], "w1b", tag="slot_d")
-        x_cols[512] = keep.tile([P, 512], U32, name="x1_hi", tag="slot_b", align_bytes=64)
-        for lo, hi in y_parts[1:]:
-            nc.vector.tensor_copy(picked_words(1, lo, hi), table1[:].indirect(entries(offs_sb, lo, hi)))
+        x_cols[0] = keep.tile([P, 768], U32, name="x1_lo", align_bytes=64)
+        nc.vector.tensor_copy(x_cols[0][:], table1[:].indirect(entries(offs_sb, 0, 768)))
+        w1q = w1q + quantize(w1b_bf[:], "w1b")
+        x_cols[768] = keep.tile([P, 256], U32, name="x1_hi", tag="slot_b", align_bytes=64)
+        nc.vector.tensor_copy(x_cols[768][:], table1[:].indirect(entries(offs_sb, 768, 1024)))
         for bank, (lo, hi) in zip(y_banks, y_parts):
-            product(bank, w1q, 1, lo, hi)
-        w2_bf = staged("w2")
-        interleave(w2_raw, w2_bf[:])
+            product(bank[:], w1q, 1, lo, hi)
+        w2_bf = staged("w2", tag="slot_d")
+        interleave(w2a_raw, w2_bf[:, 0:1])
+        interleave(w2b_raw, w2_bf[:, 1:2])
         w2q = quantize(w2_bf[:], "w2")
         y = keep.tile([P, S], F32, name="y", tag="slot_a", align_bytes=64)
         e = keep.tile([P, S], F32, name="e")
         h = keep.tile([P, S], F32, name="h")
-        nc.scalar.copy(y[:, 0:512], y_banks[0][:])
-        nc.vector.tensor_copy(y[:, 512:768], y_banks[1][:])
-        nc.vector.tensor_copy(y[:, 768:1024], y_banks[2][:])
+        for i, (bank, (lo, hi)) in enumerate(zip(y_banks, y_parts)):
+            if i % 2 == 0:
+                nc.scalar.copy(y[:, lo:hi], bank[:])
+            else:
+                nc.vector.tensor_copy(y[:, lo:hi], bank[:])
+
+        def whole_product(wq, values, tags):
+            for tag, (lo, hi), parts in zip(tags, halves, groups):
+                bank = psum.tile([P, 512], F32, name=tag, tag=tag)
+                for a, b in parts:
+                    for z in range(PASSES):
+                        product(bank[:, a - lo : b - lo], wq, z, a, b)
+                nc.scalar.copy(values[:, lo:hi], bank[:])
 
         w3_bf = staged("w3", tag="slot_d")
         interleave(w3_raw, w3_bf[:])
-        for bank, (lo, hi) in zip(e_banks, halves):
-            for z in range(PASSES):
-                product(bank, w2q, z, lo, hi)
-            nc.scalar.copy(e[:, lo:hi], bank[:])
+        whole_product(w2q, e, ("bank5", "bank6"))
 
         y_dst0 = keep.tile([P, 512], F32, name="y_dst0", align_bytes=64)
         logit = keep.tile([P, U], F32, name="logit")
@@ -175,10 +181,7 @@ def tile_picked_edgeatt_sigmoid_p_kernel(tc, x_words, x_scales, w1, w2, w3, offs
         w3q = quantize(w3_bf[:], "w3")
         y_dst1 = keep.tile([P, 512], F32, name="y_dst1", tag="slot_c", align_bytes=64)
         nc.vector.tensor_copy(y_dst1[:], y[:].indirect(entries(dst_sb, 512, 1024)))
-        for bank, (lo, hi) in zip(h_banks, halves):
-            for z in range(PASSES):
-                product(bank, w3q, z, lo, hi)
-            nc.scalar.copy(h[:, lo:hi], bank[:])
+        whole_product(w3q, h, ("bank7", "bank0"))
 
         for y_dst, (lo, hi) in zip((y_dst0, y_dst1), halves):
             nc.vector.tensor_tensor(logit[:, lo:hi], e[:].indirect(entries(src_sb, lo, hi)), y_dst[:], ADD)

@@ -46,7 +46,7 @@ def tile_picked_edgeatt_sigmoid_p_kernel(tc, x_words, x_scales, w1, w2, w3, offs
         nc.scalar.activation(warm_out[:], warm_in[:], SIGMOID)
 
         def load_scales():
-            nc.scalar.dma_start(scale_table[0:32, :].bitcast(I32), x_scales.rearrange("z r c -> r z c").bitcast(I32))
+            nc.sync.dma_start(scale_table[0:32, :].bitcast(I32), x_scales.rearrange("z r c -> r z c").bitcast(I32))
 
         def place_scales(picked):
             for q in (0, 2, 1, 3):

@@ -21,6 +21,15 @@ PACK = 4
 K_PASS = P * PACK
 PASSES = K // K_PASS
 GROUP = 16
+QUADRANT = 32
+SCALE_ROWS = 4
+BANK = 512
+
+X_SPLIT = 768
+Y_GROUPS = [(0, 256), (256, 512), (512, X_SPLIT), (X_SPLIT, 896), (896, S)]
+HALVES = [(0, BANK), (BANK, S)]
+HALF_GROUPS = [[(0, BANK)], [(BANK, X_SPLIT), (X_SPLIT, S)]]
+OUT_PIECES = [(0, 512), (512, 768), (768, 896), (896, U)]
 
 
 def tile_picked_edgeatt_sigmoid_p_kernel(tc, x_words, x_scales, w1, w2, w3, offs, src, dst, out):
@@ -35,9 +44,10 @@ def tile_picked_edgeatt_sigmoid_p_kernel(tc, x_words, x_scales, w1, w2, w3, offs
         offs_sb = keep.tile([P, S // GROUP], U16, name="offs_sb")
         dst_sb = keep.tile([P, U // GROUP], U16, name="dst_sb")
         src_sb = keep.tile([P, U // GROUP], U16, name="src_sb")
+
         scale_table = keep.tile([P, T], U8, name="scale_table", align_bytes=64)
-        nc.vector.memset(scale_table[32:64, :].bitcast(I32), 0)
-        nc.vector.memset(scale_table[64:128, :].bitcast(I32), 0)
+        nc.vector.memset(scale_table[QUADRANT : 2 * QUADRANT, :].bitcast(I32), 0)
+        nc.vector.memset(scale_table[2 * QUADRANT : P, :].bitcast(I32), 0)
         x_sc = keep.tile([P, PASSES, S], U8, name="x_sc", align_bytes=64)
         nc.vector.memset(x_sc[:].rearrange("p z s -> p (z s)").bitcast(I32), 0)
         warm_in = keep.tile([P, 1], F32, name="warm_in")
@@ -45,14 +55,12 @@ def tile_picked_edgeatt_sigmoid_p_kernel(tc, x_words, x_scales, w1, w2, w3, offs
         nc.gpsimd.memset(warm_in[:], 0.0)
         nc.scalar.activation(warm_out[:], warm_in[:], SIGMOID)
 
-        def load_scales():
-            nc.sync.dma_start(scale_table[0:32, :].bitcast(I32), x_scales.rearrange("z r c -> r z c").bitcast(I32))
-
         def place_scales(picked):
+            dense_rows = SCALE_ROWS * PASSES
             for q in (0, 2, 1, 3):
                 nc.sync.dma_start(
-                    x_sc[32 * q : 32 * q + 4].rearrange("p z s -> p (z s)").bitcast(I32),
-                    picked[8 * q : 8 * q + 8, :].bitcast(I32),
+                    x_sc[QUADRANT * q : QUADRANT * q + SCALE_ROWS].rearrange("p z s -> p (z s)").bitcast(I32),
+                    picked[dense_rows * q : dense_rows * (q + 1), :].bitcast(I32),
                 )
 
         def load_words(z):
@@ -68,36 +76,36 @@ def tile_picked_edgeatt_sigmoid_p_kernel(tc, x_words, x_scales, w1, w2, w3, offs
             )
             return raw
 
-        def interleave(raw, grouped):
+        def round_and_interleave(raw, grouped):
             nc.scalar.copy(
                 grouped.rearrange("p z (c i) j -> p z c j i", i=4),
                 raw[:].rearrange("p z j (c i) -> p z c j i", i=4),
             )
 
-        def staged(name, nz=PASSES, tag=None):
-            return keep.tile([P, nz, M, PACK], BF16, name=name + "_bf16", tag=tag or name + "_bf16", align_bytes=64)
+        def staged(name, passes=PASSES, tag=None):
+            return keep.tile([P, passes, M, PACK], BF16, name=name + "_bf16", tag=tag or name + "_bf16", align_bytes=64)
 
-        def quantize(grouped, name, tag=None):
-            nz = grouped.shape[1]
-            codes = keep.tile([P, nz * M], U32, name=name + "_codes", tag=tag or name + "_codes", align_bytes=64)
-            scales = keep.tile([P, nz * M], U8, name=name + "_scales", align_bytes=64)
+        def quantize(grouped, name):
+            passes = grouped.shape[1]
+            codes = keep.tile([P, passes * M], U32, name=name + "_codes", align_bytes=64)
+            scales = keep.tile([P, passes * M], U8, name=name + "_scales", align_bytes=64)
             nc.vector.quantize_mx(
                 out=codes[:].bitcast(FP8X4), scales=scales[:], in_=grouped.rearrange("p z m j -> p (z m j)")
             )
-            return [(codes[:, i * M : (i + 1) * M], scales[:, i * M : (i + 1) * M]) for i in range(nz)]
+            return [(codes[:, z * M : (z + 1) * M], scales[:, z * M : (z + 1) * M]) for z in range(passes)]
 
         sc_picked = keep.tile([P, S], U8, name="sc_picked", align_bytes=64)
         x0 = keep.tile([P, S], U32, name="x0", align_bytes=64)
-        x_cols = {}
+        x1_pieces = {}
 
         def picked_words(z, lo, hi):
             if z == 0:
                 return x0[:, lo:hi]
-            base = lo // 768 * 768
-            return x_cols[base][:, lo - base : hi - base]
+            first = lo // X_SPLIT * X_SPLIT
+            return x1_pieces[first][:, lo - first : hi - first]
 
-        def product(bank, wq, z, lo, hi):
-            codes, scales = wq[z]
+        def product(bank, quantized, z, lo, hi):
+            codes, scales = quantized[z]
             nc.tensor.matmul_mx(
                 out=bank,
                 lhsT=codes.bitcast(FP8X4),
@@ -108,84 +116,81 @@ def tile_picked_edgeatt_sigmoid_p_kernel(tc, x_words, x_scales, w1, w2, w3, offs
                 stop=(z == PASSES - 1),
             )
 
-        def probe(ap, name):
-            t = keep.tile([P, 1], ap.dtype, name=name)
-            nc.gpsimd.tensor_copy(t[:], ap)
 
         nc.sync.dma_start(offs_sb[:], offs)
-        load_scales()
+        nc.sync.dma_start(scale_table[0:QUADRANT, :].bitcast(I32), x_scales.rearrange("z r c -> r z c").bitcast(I32))
         table0 = load_words(0)
         w1a_raw = load_weight(w1, "w1a", 0, 1)
-        nc.sync.dma_start(dst_sb[:], dst)
-        nc.sync.dma_start(src_sb[:], src)
         table1 = load_words(1)
-        w1b_raw = load_weight(w1, "w1b", 1, 2, tag="slot_b")
+        w1b_raw = load_weight(w1, "w1b", 1, 2, tag="after_w1b_rounding")
         nc.vector.tensor_copy(sc_picked[:], scale_table[:].indirect(offs_sb[:]))
         place_scales(sc_picked)
         w2a_raw = load_weight(w2, "w2a", 0, 1)
-        w2b_raw = load_weight(w2, "w2b", 1, 2, tag="slot_a")
-        w3_raw = load_weight(w3, "w3", 0, 2, tag="slot_c")
+        w2b_raw = load_weight(w2, "w2b", 1, 2, tag="after_w2b_rounding")
+        w3_raw = keep.tile([P, PASSES, PACK, M], F32, name="w3_raw", tag="after_w3_rounding", align_bytes=64)
+        w3_rows = w3.rearrange("(z p j) m -> z p j m", p=P, j=PACK)
+        nc.sync.dma_start(w3_raw[:, 0], w3_rows[0])
+        nc.sync.dma_start(dst_sb[:], dst)
+        nc.sync.dma_start(w3_raw[:, 1], w3_rows[1])
+        nc.sync.dma_start(src_sb[:], src)
+
         nc.vector.tensor_copy(x0[:], table0[:].indirect(offs_sb[:]))
         w1a_bf = staged("w1a", 1)
-        interleave(w1a_raw, w1a_bf[:])
+        round_and_interleave(w1a_raw, w1a_bf[:])
         w1q = quantize(w1a_bf[:], "w1a")
 
-        y_parts = [(0, 256), (256, 512), (512, 768), (768, 896), (896, 1024)]
-        halves = [(0, 512), (512, 1024)]
-        groups = [[(0, 512)], [(512, 768), (768, 1024)]]
-        out_parts = [(0, 512), (512, 768), (768, 896), (896, 1024)]
-        y_banks = [psum.tile([P, hi - lo], F32, name=f"y_bank{lo}", tag=f"bank{i}") for i, (lo, hi) in enumerate(y_parts)]
-
-        for bank, (lo, hi) in zip(y_banks, y_parts):
+        y_banks = [psum.tile([P, hi - lo], F32, name=f"y_bank{lo}", tag=f"bank{i}") for i, (lo, hi) in enumerate(Y_GROUPS)]
+        for bank, (lo, hi) in zip(y_banks, Y_GROUPS):
             product(bank[:], w1q, 0, lo, hi)
 
         w1b_bf = staged("w1b", 1)
-        interleave(w1b_raw, w1b_bf[:])
-        x_cols[0] = keep.tile([P, 768], U32, name="x1_lo", align_bytes=64)
-        nc.vector.tensor_copy(x_cols[0][:], table1[:].indirect(entries(offs_sb, 0, 768)))
+        round_and_interleave(w1b_raw, w1b_bf[:])
+        x1_pieces[0] = keep.tile([P, X_SPLIT], U32, name="x1_lo", align_bytes=64)
+        nc.vector.tensor_copy(x1_pieces[0][:], table1[:].indirect(entries(offs_sb, 0, X_SPLIT)))
         w1q = w1q + quantize(w1b_bf[:], "w1b")
-        x_cols[768] = keep.tile([P, 256], U32, name="x1_hi", tag="slot_b", align_bytes=64)
-        nc.vector.tensor_copy(x_cols[768][:], table1[:].indirect(entries(offs_sb, 768, 1024)))
-        for bank, (lo, hi) in zip(y_banks, y_parts):
+        x1_pieces[X_SPLIT] = keep.tile([P, S - X_SPLIT], U32, name="x1_hi", tag="after_w1b_rounding", align_bytes=64)
+        nc.vector.tensor_copy(x1_pieces[X_SPLIT][:], table1[:].indirect(entries(offs_sb, X_SPLIT, S)))
+        for bank, (lo, hi) in zip(y_banks, Y_GROUPS):
             product(bank[:], w1q, 1, lo, hi)
-        w2_bf = staged("w2", tag="slot_d")
-        interleave(w2a_raw, w2_bf[:, 0:1])
-        interleave(w2b_raw, w2_bf[:, 1:2])
+
+        w2_bf = staged("w2", tag="after_w2_quantize")
+        round_and_interleave(w2a_raw, w2_bf[:, 0:1])
+        round_and_interleave(w2b_raw, w2_bf[:, 1:2])
         w2q = quantize(w2_bf[:], "w2")
-        y = keep.tile([P, S], F32, name="y", tag="slot_a", align_bytes=64)
+        y = keep.tile([P, S], F32, name="y", tag="after_w2b_rounding", align_bytes=64)
         e = keep.tile([P, S], F32, name="e")
         h = keep.tile([P, S], F32, name="h")
-        for i, (bank, (lo, hi)) in enumerate(zip(y_banks, y_parts)):
+        for i, (bank, (lo, hi)) in enumerate(zip(y_banks, Y_GROUPS)):
             if i % 2 == 0:
                 nc.scalar.copy(y[:, lo:hi], bank[:])
             else:
                 nc.vector.tensor_copy(y[:, lo:hi], bank[:])
 
-        def whole_product(wq, values, tags):
-            for tag, (lo, hi), parts in zip(tags, halves, groups):
-                bank = psum.tile([P, 512], F32, name=tag, tag=tag)
-                for a, b in parts:
+        def whole_product(quantized, values, bank_tags):
+            for bank_tag, (lo, hi), groups in zip(bank_tags, HALVES, HALF_GROUPS):
+                bank = psum.tile([P, BANK], F32, name=bank_tag, tag=bank_tag)
+                for first, last in groups:
                     for z in range(PASSES):
-                        product(bank[:, a - lo : b - lo], wq, z, a, b)
+                        product(bank[:, first - lo : last - lo], quantized, z, first, last)
                 nc.scalar.copy(values[:, lo:hi], bank[:])
 
-        w3_bf = staged("w3", tag="slot_d")
-        interleave(w3_raw, w3_bf[:])
+        w3_bf = staged("w3", tag="after_w2_quantize")
+        round_and_interleave(w3_raw, w3_bf[:])
         whole_product(w2q, e, ("bank5", "bank6"))
 
-        y_dst0 = keep.tile([P, 512], F32, name="y_dst0", align_bytes=64)
+        y_dst0 = keep.tile([P, BANK], F32, name="y_dst0", align_bytes=64)
         logit = keep.tile([P, U], F32, name="logit")
         gate = keep.tile([P, U], F32, name="gate")
         result = keep.tile([P, U], F32, name="result")
-        nc.vector.tensor_copy(y_dst0[:], y[:].indirect(entries(dst_sb, 0, 512)))
+        nc.vector.tensor_copy(y_dst0[:], y[:].indirect(entries(dst_sb, *HALVES[0])))
         w3q = quantize(w3_bf[:], "w3")
-        y_dst1 = keep.tile([P, 512], F32, name="y_dst1", tag="slot_c", align_bytes=64)
-        nc.vector.tensor_copy(y_dst1[:], y[:].indirect(entries(dst_sb, 512, 1024)))
+        y_dst1 = keep.tile([P, BANK], F32, name="y_dst1", tag="after_w3_rounding", align_bytes=64)
+        nc.vector.tensor_copy(y_dst1[:], y[:].indirect(entries(dst_sb, *HALVES[1])))
         whole_product(w3q, h, ("bank7", "bank0"))
 
-        for y_dst, (lo, hi) in zip((y_dst0, y_dst1), halves):
+        for y_dst, (lo, hi) in zip((y_dst0, y_dst1), HALVES):
             nc.vector.tensor_tensor(logit[:, lo:hi], e[:].indirect(entries(src_sb, lo, hi)), y_dst[:], ADD)
             nc.scalar.activation(gate[:, lo:hi], logit[:, lo:hi], SIGMOID)
-        for lo, hi in out_parts:
+        for lo, hi in OUT_PIECES:
             nc.vector.tensor_tensor(result[:, lo:hi], h[:].indirect(entries(src_sb, lo, hi)), gate[:, lo:hi], MULT)
             nc.sync.dma_start(out[:, lo:hi], result[:, lo:hi])

@@ -117,8 +117,8 @@ def tile_picked_edgeatt_sigmoid_p_kernel(tc, x_words, x_scales, w1, w2, w3, offs
             )
 
 
-        nc.sync.dma_start(offs_sb[:], offs)
         nc.sync.dma_start(scale_table[0:QUADRANT, :].bitcast(I32), x_scales.rearrange("z r c -> r z c").bitcast(I32))
+        nc.sync.dma_start(offs_sb[:], offs)
         table0 = load_words(0)
         w1a_raw = load_weight(w1, "w1a", 0, 1)
         table1 = load_words(1)

@@ -135,6 +135,17 @@ def tile_picked_edgeatt_sigmoid_p_kernel(tc, x_words, x_scales, w1, w2, w3, offs
         nc.sync.dma_start(src_sb[:], src)
 
         nc.vector.tensor_copy(x0[:], table0[:].indirect(offs_sb[:]))
+        warm_bank = psum.tile([P, BANK], F32, name="warm_bank", tag="bank7")
+        for lo, hi in HALVES:
+            nc.tensor.matmul_mx(
+                out=warm_bank[:],
+                lhsT=x0[:, 0:M].bitcast(FP8X4),
+                lhsT_scale=sc_picked[:, 0:M],
+                rhs=x0[:, lo:hi].bitcast(FP8X4),
+                rhs_scale=sc_picked[:, lo:hi],
+                start=True,
+                stop=True,
+            )
         w1a_bf = staged("w1a", 1)
         round_and_interleave(w1a_raw, w1a_bf[:])
         w1q = quantize(w1a_bf[:], "w1a")

@@ -26,10 +26,17 @@ SCALE_ROWS = 4
 BANK = 512
 
 X_SPLIT = 768
+X0_SPLIT = BANK
 Y_GROUPS = [(0, 256), (256, 512), (512, X_SPLIT), (X_SPLIT, 896), (896, S)]
+VECTOR_BANKS = (0, 1)
+W2B_AT = 512
 HALVES = [(0, BANK), (BANK, S)]
-HALF_GROUPS = [[(0, BANK)], [(BANK, X_SPLIT), (X_SPLIT, S)]]
-OUT_PIECES = [(0, 512), (512, 768), (768, 896), (896, U)]
+HALF_GROUPS = [[(lo, hi) for lo, hi in Y_GROUPS if first <= lo < last] for first, last in HALVES]
+WARM_UP_PASSES = 3
+EDGE_SPLIT = 640
+SUM_PIECES = [(0, EDGE_SPLIT), (EDGE_SPLIT, U)]
+GATE_PIECES = [(0, 256), (256, EDGE_SPLIT), (EDGE_SPLIT, U)]
+OUT_PIECES = [(0, 256), (256, EDGE_SPLIT), (EDGE_SPLIT, 896), (896, U)]
 
 
 def tile_picked_edgeatt_sigmoid_p_kernel(tc, x_words, x_scales, w1, w2, w3, offs, src, dst, out):
@@ -126,7 +133,12 @@ def tile_picked_edgeatt_sigmoid_p_kernel(tc, x_words, x_scales, w1, w2, w3, offs
         nc.vector.tensor_copy(sc_picked[:], scale_table[:].indirect(offs_sb[:]))
         place_scales(sc_picked)
         w2a_raw = load_weight(w2, "w2a", 0, 1)
-        w2b_raw = load_weight(w2, "w2b", 1, 2, tag="after_w2b_rounding")
+        y = keep.tile([P, S], F32, name="y", align_bytes=64)
+        w2b_raw = y[:, W2B_AT : W2B_AT + PACK * M].rearrange("p (z j m) -> p z j m", z=1, j=PACK)
+        nc.sync.dma_start(
+            w2b_raw.rearrange("p z j m -> p z (j m)"),
+            w2[K_PASS : 2 * K_PASS, :].rearrange("(z p j) m -> p z (j m)", p=P, j=PACK),
+        )
         w3_raw = keep.tile([P, PASSES, PACK, M], F32, name="w3_raw", tag="after_w3_rounding", align_bytes=64)
         w3_rows = w3.rearrange("(z p j) m -> z p j m", p=P, j=PACK)
         nc.sync.dma_start(w3_raw[:, 0], w3_rows[0])
@@ -134,15 +146,16 @@ def tile_picked_edgeatt_sigmoid_p_kernel(tc, x_words, x_scales, w1, w2, w3, offs
         nc.sync.dma_start(w3_raw[:, 1], w3_rows[1])
         nc.sync.dma_start(src_sb[:], src)
 
-        nc.vector.tensor_copy(x0[:], table0[:].indirect(offs_sb[:]))
+        for lo, hi in ((0, X0_SPLIT), (X0_SPLIT, S)):
+            nc.vector.tensor_copy(x0[:, lo:hi], table0[:].indirect(entries(offs_sb, lo, hi)))
         warm_bank = psum.tile([P, BANK], F32, name="warm_bank", tag="bank7")
-        for lo, hi in HALVES:
+        for turn in range(WARM_UP_PASSES):
             nc.tensor.matmul_mx(
                 out=warm_bank[:],
                 lhsT=x0[:, 0:M].bitcast(FP8X4),
                 lhsT_scale=sc_picked[:, 0:M],
-                rhs=x0[:, lo:hi].bitcast(FP8X4),
-                rhs_scale=sc_picked[:, lo:hi],
+                rhs=x0[:, 0:BANK].bitcast(FP8X4),
+                rhs_scale=sc_picked[:, 0:BANK],
                 start=True,
                 stop=True,
             )
@@ -168,14 +181,13 @@ def tile_picked_edgeatt_sigmoid_p_kernel(tc, x_words, x_scales, w1, w2, w3, offs
         round_and_interleave(w2a_raw, w2_bf[:, 0:1])
         round_and_interleave(w2b_raw, w2_bf[:, 1:2])
         w2q = quantize(w2_bf[:], "w2")
-        y = keep.tile([P, S], F32, name="y", tag="after_w2b_rounding", align_bytes=64)
         e = keep.tile([P, S], F32, name="e")
         h = keep.tile([P, S], F32, name="h")
         for i, (bank, (lo, hi)) in enumerate(zip(y_banks, Y_GROUPS)):
-            if i % 2 == 0:
-                nc.scalar.copy(y[:, lo:hi], bank[:])
-            else:
+            if i in VECTOR_BANKS:
                 nc.vector.tensor_copy(y[:, lo:hi], bank[:])
+            else:
+                nc.scalar.copy(y[:, lo:hi], bank[:])
 
         def whole_product(quantized, values, bank_tags):
             for bank_tag, (lo, hi), groups in zip(bank_tags, HALVES, HALF_GROUPS):
@@ -189,18 +201,19 @@ def tile_picked_edgeatt_sigmoid_p_kernel(tc, x_words, x_scales, w1, w2, w3, offs
         round_and_interleave(w3_raw, w3_bf[:])
         whole_product(w2q, e, ("bank5", "bank6"))
 
-        y_dst0 = keep.tile([P, BANK], F32, name="y_dst0", align_bytes=64)
+        y_dst0 = keep.tile([P, EDGE_SPLIT], F32, name="y_dst0", align_bytes=64)
         logit = keep.tile([P, U], F32, name="logit")
         gate = keep.tile([P, U], F32, name="gate")
         result = keep.tile([P, U], F32, name="result")
-        nc.vector.tensor_copy(y_dst0[:], y[:].indirect(entries(dst_sb, *HALVES[0])))
+        nc.vector.tensor_copy(y_dst0[:], y[:].indirect(entries(dst_sb, *SUM_PIECES[0])))
         w3q = quantize(w3_bf[:], "w3")
-        y_dst1 = keep.tile([P, BANK], F32, name="y_dst1", tag="after_w3_rounding", align_bytes=64)
-        nc.vector.tensor_copy(y_dst1[:], y[:].indirect(entries(dst_sb, *HALVES[1])))
+        y_dst1 = keep.tile([P, U - EDGE_SPLIT], F32, name="y_dst1", tag="after_w3_rounding", align_bytes=64)
+        nc.vector.tensor_copy(y_dst1[:], y[:].indirect(entries(dst_sb, *SUM_PIECES[1])))
         whole_product(w3q, h, ("bank7", "bank0"))
 
-        for y_dst, (lo, hi) in zip((y_dst0, y_dst1), HALVES):
+        for y_dst, (lo, hi) in zip((y_dst0, y_dst1), SUM_PIECES):
             nc.vector.tensor_tensor(logit[:, lo:hi], e[:].indirect(entries(src_sb, lo, hi)), y_dst[:], ADD)
+        for lo, hi in GATE_PIECES:
             nc.scalar.activation(gate[:, lo:hi], logit[:, lo:hi], SIGMOID)
         for lo, hi in OUT_PIECES:
             nc.vector.tensor_tensor(result[:, lo:hi], h[:].indirect(entries(src_sb, lo, hi)), gate[:, lo:hi], MULT)

@@ -26,7 +26,7 @@ SCALE_ROWS = 4
 BANK = 512
 
 X_SPLIT = 768
-X0_SPLIT = BANK
+X0_SPLIT = 768
 Y_GROUPS = [(0, 256), (256, 512), (512, X_SPLIT), (X_SPLIT, 896), (896, S)]
 VECTOR_BANKS = (0, 1)
 W2B_AT = 512

@@ -85,8 +85,8 @@ def tile_picked_edgeatt_sigmoid_p_kernel(tc, x_words, x_scales, w1, w2, w3, offs
 
         def round_and_interleave(raw, grouped):
             nc.scalar.copy(
-                grouped.rearrange("p z (c i) j -> p z c j i", i=4),
-                raw[:].rearrange("p z j (c i) -> p z c j i", i=4),
+                grouped.rearrange("p z (c i) j -> p z c j i", i=2),
+                raw[:].rearrange("p z j (c i) -> p z c j i", i=2),
             )
 
         def staged(name, passes=PASSES, tag=None):

@@ -15,6 +15,7 @@ FP8X4 = mybir.dt.float8_e4m3fn_x4
 ADD = mybir.AluOpType.add
 MULT = mybir.AluOpType.mult
 SIGMOID = mybir.ActivationFunctionType.Sigmoid
+COPY = mybir.ActivationFunctionType.Copy
 
 P = 128
 PACK = 4
@@ -26,17 +27,14 @@ SCALE_ROWS = 4
 BANK = 512
 
 X_SPLIT = 768
-X0_SPLIT = 768
-Y_GROUPS = [(0, 256), (256, 512), (512, X_SPLIT), (X_SPLIT, 896), (896, S)]
-VECTOR_BANKS = (0, 1)
-W2B_AT = 512
 HALVES = [(0, BANK), (BANK, S)]
-HALF_GROUPS = [[(lo, hi) for lo, hi in Y_GROUPS if first <= lo < last] for first, last in HALVES]
-WARM_UP_PASSES = 3
-EDGE_SPLIT = 640
-SUM_PIECES = [(0, EDGE_SPLIT), (EDGE_SPLIT, U)]
-GATE_PIECES = [(0, 256), (256, EDGE_SPLIT), (EDGE_SPLIT, U)]
-OUT_PIECES = [(0, 256), (256, EDGE_SPLIT), (EDGE_SPLIT, 896), (896, U)]
+Y_GROUPS = [(0, BANK), (BANK, X_SPLIT), (X_SPLIT, S)]
+W2B_AT = 480
+DST_SPLIT = 320
+SRC_SPLIT = 576
+SUM_PIECES = [(0, DST_SPLIT), (DST_SPLIT, 640), (640, U)]
+GATE_PIECES = SUM_PIECES
+OUT_PIECES = [(0, DST_SPLIT), (DST_SPLIT, SRC_SPLIT), (SRC_SPLIT, 832), (832, U)]
 
 
 def tile_picked_edgeatt_sigmoid_p_kernel(tc, x_words, x_scales, w1, w2, w3, offs, src, dst, out):
@@ -75,26 +73,27 @@ def tile_picked_edgeatt_sigmoid_p_kernel(tc, x_words, x_scales, w1, w2, w3, offs
             nc.sync.dma_start(table[:].bitcast(I32), x_words[z].rearrange("p n t -> p (n t)").bitcast(I32))
             return table
 
-        def load_weight(w, name, z0, z1, tag=None):
-            raw = keep.tile([P, z1 - z0, PACK, M], F32, name=name + "_raw", tag=tag or name + "_raw", align_bytes=64)
+        def load_pass(raw, w, z):
             nc.sync.dma_start(
-                raw[:].rearrange("p z j m -> p z (j m)"),
-                w[z0 * K_PASS : z1 * K_PASS, :].rearrange("(z p j) m -> p z (j m)", p=P, j=PACK),
-            )
-            return raw
-
-        def round_and_interleave(raw, grouped):
-            nc.scalar.copy(
-                grouped.rearrange("p z (c i) j -> p z c j i", i=2),
-                raw[:].rearrange("p z j (c i) -> p z c j i", i=2),
+                raw.rearrange("p j m -> p (j m)"),
+                w[z * K_PASS : (z + 1) * K_PASS, :].rearrange("(p j) m -> p (j m)", j=PACK),
             )
 
-        def staged(name, passes=PASSES, tag=None):
+        def raw_tile(name, tag=None):
+            return keep.tile([P, PACK, M], F32, name=name + "_raw", tag=tag or name + "_raw", align_bytes=64)
+
+        def walk_out(grouped):
+            return grouped.rearrange("p (c i) j -> p c j i", i=2)
+
+        def walk_in(raw):
+            return raw.rearrange("p j (c i) -> p c j i", i=2)
+
+        def staged(name, passes=1, tag=None):
             return keep.tile([P, passes, M, PACK], BF16, name=name + "_bf16", tag=tag or name + "_bf16", align_bytes=64)
 
         def quantize(grouped, name):
             passes = grouped.shape[1]
-            codes = keep.tile([P, passes * M], U32, name=name + "_codes", align_bytes=64)
+            codes = keep.tile([P, passes * M], U32, name=name + "_codes", tag=name + "_codes", align_bytes=64)
             scales = keep.tile([P, passes * M], U8, name=name + "_scales", align_bytes=64)
             nc.vector.quantize_mx(
                 out=codes[:].bitcast(FP8X4), scales=scales[:], in_=grouped.rearrange("p z m j -> p (z m j)")
@@ -111,110 +110,119 @@ def tile_picked_edgeatt_sigmoid_p_kernel(tc, x_words, x_scales, w1, w2, w3, offs
             first = lo // X_SPLIT * X_SPLIT
             return x1_pieces[first][:, lo - first : hi - first]
 
-        def product(bank, quantized, z, lo, hi):
-            codes, scales = quantized[z]
+        def product(bank, quantized, z, lo, hi, start, stop):
+            codes, scales = quantized
             nc.tensor.matmul_mx(
                 out=bank,
                 lhsT=codes.bitcast(FP8X4),
                 lhsT_scale=scales,
                 rhs=picked_words(z, lo, hi).bitcast(FP8X4),
                 rhs_scale=x_sc[:, z, lo:hi],
-                start=(z == 0),
-                stop=(z == PASSES - 1),
+                start=start,
+                stop=stop,
             )
 
+        def banks(name, groups, tags):
+            return [(psum.tile([P, hi - lo], F32, name=f"{name}_bank{lo}", tag=tag), lo, hi) for (lo, hi), tag in zip(groups, tags)]
+
+        def first_pass(group_banks, quantized):
+            for bank, lo, hi in group_banks:
+                product(bank[:], quantized, 0, lo, hi, True, False)
+
+        def second_pass(group_banks, quantized):
+            for bank, first, last in group_banks:
+                cuts = [(first, X_SPLIT), (X_SPLIT, last)] if first < X_SPLIT < last else [(first, last)]
+                for lo, hi in cuts:
+                    product(bank[:, lo - first : hi - first], quantized, 1, lo, hi, False, hi == last)
 
         nc.sync.dma_start(scale_table[0:QUADRANT, :].bitcast(I32), x_scales.rearrange("z r c -> r z c").bitcast(I32))
         nc.sync.dma_start(offs_sb[:], offs)
         table0 = load_words(0)
-        w1a_raw = load_weight(w1, "w1a", 0, 1)
+        w1a_raw = raw_tile("w1a")
+        load_pass(w1a_raw[:], w1, 0)
         table1 = load_words(1)
-        w1b_raw = load_weight(w1, "w1b", 1, 2, tag="after_w1b_rounding")
+        w1b_raw = raw_tile("w1b", tag="after_w1b_rounding")
+        load_pass(w1b_raw[:], w1, 1)
         nc.vector.tensor_copy(sc_picked[:], scale_table[:].indirect(offs_sb[:]))
         place_scales(sc_picked)
-        w2a_raw = load_weight(w2, "w2a", 0, 1)
+        w2a_raw = raw_tile("w2a")
+        load_pass(w2a_raw[:], w2, 0)
         y = keep.tile([P, S], F32, name="y", align_bytes=64)
-        w2b_raw = y[:, W2B_AT : W2B_AT + PACK * M].rearrange("p (z j m) -> p z j m", z=1, j=PACK)
-        nc.sync.dma_start(
-            w2b_raw.rearrange("p z j m -> p z (j m)"),
-            w2[K_PASS : 2 * K_PASS, :].rearrange("(z p j) m -> p z (j m)", p=P, j=PACK),
-        )
-        w3_raw = keep.tile([P, PASSES, PACK, M], F32, name="w3_raw", tag="after_w3_rounding", align_bytes=64)
-        w3_rows = w3.rearrange("(z p j) m -> z p j m", p=P, j=PACK)
-        nc.sync.dma_start(w3_raw[:, 0], w3_rows[0])
+        w2b_raw = y[:, W2B_AT : W2B_AT + PACK * M].rearrange("p (j m) -> p j m", j=PACK)
+        load_pass(w2b_raw, w2, 1)
+        w3a_raw = raw_tile("w3a")
+        load_pass(w3a_raw[:], w3, 0)
+        w3b_raw = raw_tile("w3b", tag="after_w3b_rounding")
+        load_pass(w3b_raw[:], w3, 1)
         nc.sync.dma_start(dst_sb[:], dst)
-        nc.sync.dma_start(w3_raw[:, 1], w3_rows[1])
         nc.sync.dma_start(src_sb[:], src)
 
-        for lo, hi in ((0, X0_SPLIT), (X0_SPLIT, S)):
-            nc.vector.tensor_copy(x0[:, lo:hi], table0[:].indirect(entries(offs_sb, lo, hi)))
-        warm_bank = psum.tile([P, BANK], F32, name="warm_bank", tag="bank7")
-        for turn in range(WARM_UP_PASSES):
-            nc.tensor.matmul_mx(
-                out=warm_bank[:],
-                lhsT=x0[:, 0:M].bitcast(FP8X4),
-                lhsT_scale=sc_picked[:, 0:M],
-                rhs=x0[:, 0:BANK].bitcast(FP8X4),
-                rhs_scale=sc_picked[:, 0:BANK],
-                start=True,
-                stop=True,
-            )
-        w1a_bf = staged("w1a", 1)
-        round_and_interleave(w1a_raw, w1a_bf[:])
-        w1q = quantize(w1a_bf[:], "w1a")
+        nc.vector.tensor_copy(x0[:], table0[:].indirect(offs_sb[:]))
+        w1a_bf = staged("w1a")
+        nc.scalar.copy(walk_out(w1a_bf[:, 0]), walk_in(w1a_raw[:]))
+        (w1a_q,) = quantize(w1a_bf[:], "w1a")
+        y_banks = banks("y", Y_GROUPS, ("bank0", "bank1", "bank2"))
+        first_pass(y_banks, w1a_q)
 
-        y_banks = [psum.tile([P, hi - lo], F32, name=f"y_bank{lo}", tag=f"bank{i}") for i, (lo, hi) in enumerate(Y_GROUPS)]
-        for bank, (lo, hi) in zip(y_banks, Y_GROUPS):
-            product(bank[:], w1q, 0, lo, hi)
-
-        w1b_bf = staged("w1b", 1)
-        round_and_interleave(w1b_raw, w1b_bf[:])
+        w1b_bf = staged("w1b")
+        nc.scalar.copy(walk_out(w1b_bf[:, 0]), walk_in(w1b_raw[:]))
         x1_pieces[0] = keep.tile([P, X_SPLIT], U32, name="x1_lo", align_bytes=64)
         nc.vector.tensor_copy(x1_pieces[0][:], table1[:].indirect(entries(offs_sb, 0, X_SPLIT)))
-        w1q = w1q + quantize(w1b_bf[:], "w1b")
+        (w1b_q,) = quantize(w1b_bf[:], "w1b")
         x1_pieces[X_SPLIT] = keep.tile([P, S - X_SPLIT], U32, name="x1_hi", tag="after_w1b_rounding", align_bytes=64)
         nc.vector.tensor_copy(x1_pieces[X_SPLIT][:], table1[:].indirect(entries(offs_sb, X_SPLIT, S)))
-        for bank, (lo, hi) in zip(y_banks, Y_GROUPS):
-            product(bank[:], w1q, 1, lo, hi)
+        second_pass(y_banks, w1b_q)
 
-        w2_bf = staged("w2", tag="after_w2_quantize")
-        round_and_interleave(w2a_raw, w2_bf[:, 0:1])
-        round_and_interleave(w2b_raw, w2_bf[:, 1:2])
-        w2q = quantize(w2_bf[:], "w2")
+        w2_bf = staged("w2", PASSES, tag="after_w2b_quantize")
+        nc.scalar.copy(walk_out(w2_bf[:, 0]), walk_in(w2a_raw[:]))
+        nc.scalar.copy(walk_out(w2_bf[:, 1]), walk_in(w2b_raw))
+        w2a_q, w2b_q = quantize(w2_bf[:], "w2")
+        for bank, lo, hi in y_banks[:-1]:
+            nc.scalar.copy(y[:, lo:hi], bank[:])
+
+        e_banks = banks("e", HALVES, ("bank3", "bank4"))
+        for bank in e_banks:
+            first_pass([bank], w2a_q)
+            second_pass([bank], w2b_q)
+
+        w3a_bf = staged("w3a", tag="after_w2b_quantize")
+        nc.vector.tensor_copy(walk_out(w3a_bf[:, 0]), walk_in(w3a_raw[:]))
+        bank, lo, hi = y_banks[-1]
+        nc.vector.tensor_copy(y[:, lo:hi], bank[:])
+        w3b_bf = staged("w3b")
+        nc.vector.tensor_copy(walk_out(w3b_bf[:, 0]), walk_in(w3b_raw[:]))
+        w3_q = quantize(w3a_bf[:], "w3a") + quantize(w3b_bf[:], "w3b")
         e = keep.tile([P, S], F32, name="e")
         h = keep.tile([P, S], F32, name="h")
-        for i, (bank, (lo, hi)) in enumerate(zip(y_banks, Y_GROUPS)):
-            if i in VECTOR_BANKS:
-                nc.vector.tensor_copy(y[:, lo:hi], bank[:])
-            else:
-                nc.scalar.copy(y[:, lo:hi], bank[:])
+        for bank, lo, hi in e_banks:
+            nc.scalar.copy(e[:, lo:hi], bank[:])
+        h_banks = banks("h", HALVES, ("bank5", "bank6"))
+        for bank in h_banks:
+            first_pass([bank], w3_q[0])
+            second_pass([bank], w3_q[1])
 
-        def whole_product(quantized, values, bank_tags):
-            for bank_tag, (lo, hi), groups in zip(bank_tags, HALVES, HALF_GROUPS):
-                bank = psum.tile([P, BANK], F32, name=bank_tag, tag=bank_tag)
-                for first, last in groups:
-                    for z in range(PASSES):
-                        product(bank[:, first - lo : last - lo], quantized, z, first, last)
-                nc.scalar.copy(values[:, lo:hi], bank[:])
-
-        w3_bf = staged("w3", tag="after_w2_quantize")
-        round_and_interleave(w3_raw, w3_bf[:])
-        whole_product(w2q, e, ("bank5", "bank6"))
-
-        y_dst0 = keep.tile([P, EDGE_SPLIT], F32, name="y_dst0", align_bytes=64)
+        y_dst0 = keep.tile([P, DST_SPLIT], F32, name="y_dst0", tag="after_w3b_rounding", align_bytes=64)
+        y_dst1 = keep.tile([P, U - DST_SPLIT], F32, name="y_dst1", tag="w2_codes", align_bytes=64)
         logit = keep.tile([P, U], F32, name="logit")
         gate = keep.tile([P, U], F32, name="gate")
+        h_src = keep.tile([P, U - SRC_SPLIT], F32, name="h_src")
         result = keep.tile([P, U], F32, name="result")
-        nc.vector.tensor_copy(y_dst0[:], y[:].indirect(entries(dst_sb, *SUM_PIECES[0])))
-        w3q = quantize(w3_bf[:], "w3")
-        y_dst1 = keep.tile([P, U - EDGE_SPLIT], F32, name="y_dst1", tag="after_w3_rounding", align_bytes=64)
-        nc.vector.tensor_copy(y_dst1[:], y[:].indirect(entries(dst_sb, *SUM_PIECES[1])))
-        whole_product(w3q, h, ("bank7", "bank0"))
-
-        for y_dst, (lo, hi) in zip((y_dst0, y_dst1), SUM_PIECES):
-            nc.vector.tensor_tensor(logit[:, lo:hi], e[:].indirect(entries(src_sb, lo, hi)), y_dst[:], ADD)
+        nc.vector.tensor_copy(y_dst0[:], y[:].indirect(entries(dst_sb, 0, DST_SPLIT)))
+        for lo, hi in SUM_PIECES[1:]:
+            nc.scalar.activation(y_dst1[:, lo - DST_SPLIT : hi - DST_SPLIT], y[:].indirect(entries(dst_sb, lo, hi)), COPY)
+        for bank, lo, hi in h_banks:
+            nc.scalar.copy(h[:, lo:hi], bank[:])
+        for lo, hi in SUM_PIECES:
+            y_dst = y_dst0[:] if lo < DST_SPLIT else y_dst1[:, lo - DST_SPLIT : hi - DST_SPLIT]
+            nc.vector.tensor_tensor(logit[:, lo:hi], e[:].indirect(entries(src_sb, lo, hi)), y_dst, ADD)
         for lo, hi in GATE_PIECES:
             nc.scalar.activation(gate[:, lo:hi], logit[:, lo:hi], SIGMOID)
+        for lo, hi in OUT_PIECES[2:]:
+            nc.scalar.activation(h_src[:, lo - SRC_SPLIT : hi - SRC_SPLIT], h[:].indirect(entries(src_sb, lo, hi)), COPY)
         for lo, hi in OUT_PIECES:
-            nc.vector.tensor_tensor(result[:, lo:hi], h[:].indirect(entries(src_sb, lo, hi)), gate[:, lo:hi], MULT)
+            if lo < SRC_SPLIT:
+                picked_h = h[:].indirect(entries(src_sb, lo, hi))
+            else:
+                picked_h = h_src[:, lo - SRC_SPLIT : hi - SRC_SPLIT]
+            nc.vector.tensor_tensor(result[:, lo:hi], picked_h, gate[:, lo:hi], MULT)
             nc.sync.dma_start(out[:, lo:hi], result[:, lo:hi])

@@ -28,8 +28,7 @@ BANK = 512
 
 X_SPLIT = 768
 HALVES = [(0, BANK), (BANK, S)]
-Y_GROUPS = [(0, BANK), (BANK, X_SPLIT), (X_SPLIT, S)]
-W2B_AT = 480
+PASS_CUTS = [0, 512, X_SPLIT, S]
 DST_SPLIT = 320
 SRC_SPLIT = 576
 SUM_PIECES = [(0, DST_SPLIT), (DST_SPLIT, 640), (640, U)]
@@ -107,7 +106,7 @@ def tile_picked_edgeatt_sigmoid_p_kernel(tc, x_words, x_scales, w1, w2, w3, offs
         def picked_words(z, lo, hi):
             if z == 0:
                 return x0[:, lo:hi]
-            first = lo // X_SPLIT * X_SPLIT
+            first = 0 if lo < X_SPLIT else X_SPLIT
             return x1_pieces[first][:, lo - first : hi - first]
 
         def product(bank, quantized, z, lo, hi, start, stop):
@@ -131,8 +130,8 @@ def tile_picked_edgeatt_sigmoid_p_kernel(tc, x_words, x_scales, w1, w2, w3, offs
 
         def second_pass(group_banks, quantized):
             for bank, first, last in group_banks:
-                cuts = [(first, X_SPLIT), (X_SPLIT, last)] if first < X_SPLIT < last else [(first, last)]
-                for lo, hi in cuts:
+                cuts = [cut for cut in PASS_CUTS if first <= cut <= last]
+                for lo, hi in zip(cuts, cuts[1:]):
                     product(bank[:, lo - first : hi - first], quantized, 1, lo, hi, False, hi == last)
 
         nc.sync.dma_start(scale_table[0:QUADRANT, :].bitcast(I32), x_scales.rearrange("z r c -> r z c").bitcast(I32))
@@ -141,15 +140,14 @@ def tile_picked_edgeatt_sigmoid_p_kernel(tc, x_words, x_scales, w1, w2, w3, offs
         w1a_raw = raw_tile("w1a")
         load_pass(w1a_raw[:], w1, 0)
         table1 = load_words(1)
-        w1b_raw = raw_tile("w1b", tag="after_w1b_rounding")
-        load_pass(w1b_raw[:], w1, 1)
         nc.vector.tensor_copy(sc_picked[:], scale_table[:].indirect(offs_sb[:]))
         place_scales(sc_picked)
+        w1b_raw = raw_tile("w1b", tag="after_w1b_rounding")
+        load_pass(w1b_raw[:], w1, 1)
         w2a_raw = raw_tile("w2a")
         load_pass(w2a_raw[:], w2, 0)
-        y = keep.tile([P, S], F32, name="y", align_bytes=64)
-        w2b_raw = y[:, W2B_AT : W2B_AT + PACK * M].rearrange("p (j m) -> p j m", j=PACK)
-        load_pass(w2b_raw, w2, 1)
+        w2b_raw = raw_tile("w2b")
+        load_pass(w2b_raw[:], w2, 1)
         w3a_raw = raw_tile("w3a")
         load_pass(w3a_raw[:], w3, 0)
         w3b_raw = raw_tile("w3b", tag="after_w3b_rounding")
@@ -161,7 +159,7 @@ def tile_picked_edgeatt_sigmoid_p_kernel(tc, x_words, x_scales, w1, w2, w3, offs
         w1a_bf = staged("w1a")
         nc.scalar.copy(walk_out(w1a_bf[:, 0]), walk_in(w1a_raw[:]))
         (w1a_q,) = quantize(w1a_bf[:], "w1a")
-        y_banks = banks("y", Y_GROUPS, ("bank0", "bank1", "bank2"))
+        y_banks = banks("y", HALVES, ("bank0", "bank1"))
         first_pass(y_banks, w1a_q)
 
         w1b_bf = staged("w1b")
@@ -173,11 +171,14 @@ def tile_picked_edgeatt_sigmoid_p_kernel(tc, x_words, x_scales, w1, w2, w3, offs
         nc.vector.tensor_copy(x1_pieces[X_SPLIT][:], table1[:].indirect(entries(offs_sb, X_SPLIT, S)))
         second_pass(y_banks, w1b_q)
 
-        w2_bf = staged("w2", PASSES, tag="after_w2b_quantize")
-        nc.scalar.copy(walk_out(w2_bf[:, 0]), walk_in(w2a_raw[:]))
-        nc.scalar.copy(walk_out(w2_bf[:, 1]), walk_in(w2b_raw))
-        w2a_q, w2b_q = quantize(w2_bf[:], "w2")
-        for bank, lo, hi in y_banks[:-1]:
+        w2a_bf = staged("w2a")
+        nc.scalar.copy(walk_out(w2a_bf[:, 0]), walk_in(w2a_raw[:]))
+        w2b_bf = staged("w2b", tag="after_w2b_quantize")
+        nc.vector.tensor_copy(w2b_bf[:, 0], w2b_raw[:].rearrange("p j m -> p m j"))
+        (w2a_q,) = quantize(w2a_bf[:], "w2a")
+        (w2b_q,) = quantize(w2b_bf[:], "w2b")
+        y = keep.tile([P, S], F32, name="y", align_bytes=64)
+        for bank, lo, hi in y_banks:
             nc.scalar.copy(y[:, lo:hi], bank[:])
 
         e_banks = banks("e", HALVES, ("bank3", "bank4"))
@@ -186,11 +187,9 @@ def tile_picked_edgeatt_sigmoid_p_kernel(tc, x_words, x_scales, w1, w2, w3, offs
             second_pass([bank], w2b_q)
 
         w3a_bf = staged("w3a", tag="after_w2b_quantize")
-        nc.vector.tensor_copy(walk_out(w3a_bf[:, 0]), walk_in(w3a_raw[:]))
-        bank, lo, hi = y_banks[-1]
-        nc.vector.tensor_copy(y[:, lo:hi], bank[:])
+        nc.vector.tensor_copy(w3a_bf[:, 0], w3a_raw[:].rearrange("p j m -> p m j"))
         w3b_bf = staged("w3b")
-        nc.vector.tensor_copy(walk_out(w3b_bf[:, 0]), walk_in(w3b_raw[:]))
+        nc.vector.tensor_copy(w3b_bf[:, 0], w3b_raw[:].rearrange("p j m -> p m j"))
         w3_q = quantize(w3a_bf[:], "w3a") + quantize(w3b_bf[:], "w3b")
         e = keep.tile([P, S], F32, name="e")
         h = keep.tile([P, S], F32, name="h")
@@ -202,7 +201,7 @@ def tile_picked_edgeatt_sigmoid_p_kernel(tc, x_words, x_scales, w1, w2, w3, offs
             second_pass([bank], w3_q[1])
 
         y_dst0 = keep.tile([P, DST_SPLIT], F32, name="y_dst0", tag="after_w3b_rounding", align_bytes=64)
-        y_dst1 = keep.tile([P, U - DST_SPLIT], F32, name="y_dst1", tag="w2_codes", align_bytes=64)
+        y_dst1 = keep.tile([P, U - DST_SPLIT], F32, name="y_dst1", tag="w2b_codes", align_bytes=64)
         logit = keep.tile([P, U], F32, name="logit")
         gate = keep.tile([P, U], F32, name="gate")
         h_src = keep.tile([P, U - SRC_SPLIT], F32, name="h_src")

@@ -29,11 +29,11 @@ BANK = 512
 X_SPLIT = 768
 HALVES = [(0, BANK), (BANK, S)]
 PASS_CUTS = [0, 512, X_SPLIT, S]
-DST_SPLIT = 320
-SRC_SPLIT = 576
-SUM_PIECES = [(0, DST_SPLIT), (DST_SPLIT, 640), (640, U)]
-GATE_PIECES = SUM_PIECES
-OUT_PIECES = [(0, DST_SPLIT), (DST_SPLIT, SRC_SPLIT), (SRC_SPLIT, 832), (832, U)]
+DST_SPLIT = 448
+SRC_SPLIT = 704
+SUM_PIECES = [(0, DST_SPLIT), (DST_SPLIT, SRC_SPLIT), (SRC_SPLIT, U)]
+GATE_PIECES = [(0, 320), (320, SRC_SPLIT), (SRC_SPLIT, U)]
+OUT_PIECES = [(0, 320), (320, SRC_SPLIT), (SRC_SPLIT, 896), (896, U)]
 
 
 def tile_picked_edgeatt_sigmoid_p_kernel(tc, x_words, x_scales, w1, w2, w3, offs, src, dst, out):
@@ -52,19 +52,17 @@ def tile_picked_edgeatt_sigmoid_p_kernel(tc, x_words, x_scales, w1, w2, w3, offs
         scale_table = keep.tile([P, T], U8, name="scale_table", align_bytes=64)
         nc.vector.memset(scale_table[QUADRANT : 2 * QUADRANT, :].bitcast(I32), 0)
         nc.vector.memset(scale_table[2 * QUADRANT : P, :].bitcast(I32), 0)
-        x_sc = keep.tile([P, PASSES, S], U8, name="x_sc", align_bytes=64)
-        nc.vector.memset(x_sc[:].rearrange("p z s -> p (z s)").bitcast(I32), 0)
+        x_sc = keep.tile([P, S], U8, name="x_sc", align_bytes=64)
         warm_in = keep.tile([P, 1], F32, name="warm_in")
         warm_out = keep.tile([P, 1], F32, name="warm_out")
         nc.gpsimd.memset(warm_in[:], 0.0)
         nc.scalar.activation(warm_out[:], warm_in[:], SIGMOID)
 
         def place_scales(picked):
-            dense_rows = SCALE_ROWS * PASSES
-            for q in (0, 2, 1, 3):
+            for r in range(SCALE_ROWS):
                 nc.sync.dma_start(
-                    x_sc[QUADRANT * q : QUADRANT * q + SCALE_ROWS].rearrange("p z s -> p (z s)").bitcast(I32),
-                    picked[dense_rows * q : dense_rows * (q + 1), :].bitcast(I32),
+                    x_sc[r:P:SCALE_ROWS, :].bitcast(I32),
+                    picked[PASSES * r : PASSES * r + QUADRANT, :].bitcast(I32),
                 )
 
         def load_words(z):
@@ -116,7 +114,7 @@ def tile_picked_edgeatt_sigmoid_p_kernel(tc, x_words, x_scales, w1, w2, w3, offs
                 lhsT=codes.bitcast(FP8X4),
                 lhsT_scale=scales,
                 rhs=picked_words(z, lo, hi).bitcast(FP8X4),
-                rhs_scale=x_sc[:, z, lo:hi],
+                rhs_scale=x_sc[SCALE_ROWS * z : P, lo:hi],
                 start=start,
                 stop=stop,
             )
@@ -140,17 +138,17 @@ def tile_picked_edgeatt_sigmoid_p_kernel(tc, x_words, x_scales, w1, w2, w3, offs
         w1a_raw = raw_tile("w1a")
         load_pass(w1a_raw[:], w1, 0)
         table1 = load_words(1)
-        nc.vector.tensor_copy(sc_picked[:], scale_table[:].indirect(offs_sb[:]))
-        place_scales(sc_picked)
         w1b_raw = raw_tile("w1b", tag="after_w1b_rounding")
         load_pass(w1b_raw[:], w1, 1)
+        nc.vector.tensor_copy(sc_picked[:], scale_table[:].indirect(offs_sb[:]))
+        place_scales(sc_picked)
         w2a_raw = raw_tile("w2a")
         load_pass(w2a_raw[:], w2, 0)
         w2b_raw = raw_tile("w2b")
         load_pass(w2b_raw[:], w2, 1)
         w3a_raw = raw_tile("w3a")
         load_pass(w3a_raw[:], w3, 0)
-        w3b_raw = raw_tile("w3b", tag="after_w3b_rounding")
+        w3b_raw = raw_tile("w3b")
         load_pass(w3b_raw[:], w3, 1)
         nc.sync.dma_start(dst_sb[:], dst)
         nc.sync.dma_start(src_sb[:], src)
@@ -173,7 +171,7 @@ def tile_picked_edgeatt_sigmoid_p_kernel(tc, x_words, x_scales, w1, w2, w3, offs
 
         w2a_bf = staged("w2a")
         nc.scalar.copy(walk_out(w2a_bf[:, 0]), walk_in(w2a_raw[:]))
-        w2b_bf = staged("w2b", tag="after_w2b_quantize")
+        w2b_bf = staged("w2b")
         nc.vector.tensor_copy(w2b_bf[:, 0], w2b_raw[:].rearrange("p j m -> p m j"))
         (w2a_q,) = quantize(w2a_bf[:], "w2a")
         (w2b_q,) = quantize(w2b_bf[:], "w2b")
@@ -186,11 +184,12 @@ def tile_picked_edgeatt_sigmoid_p_kernel(tc, x_words, x_scales, w1, w2, w3, offs
             first_pass([bank], w2a_q)
             second_pass([bank], w2b_q)
 
-        w3a_bf = staged("w3a", tag="after_w2b_quantize")
-        nc.vector.tensor_copy(w3a_bf[:, 0], w3a_raw[:].rearrange("p j m -> p m j"))
-        w3b_bf = staged("w3b")
-        nc.vector.tensor_copy(w3b_bf[:, 0], w3b_raw[:].rearrange("p j m -> p m j"))
-        w3_q = quantize(w3a_bf[:], "w3a") + quantize(w3b_bf[:], "w3b")
+        w3_bf = staged("w3", PASSES)
+        for z, raw in enumerate((w3a_raw, w3b_raw)):
+            nc.vector.tensor_copy(w3_bf[:, z], raw[:].rearrange("p j m -> p m j"))
+        y_dst0 = keep.tile([P, DST_SPLIT], F32, name="y_dst0", align_bytes=64)
+        nc.vector.tensor_copy(y_dst0[:], y[:].indirect(entries(dst_sb, 0, DST_SPLIT)))
+        w3_q = quantize(w3_bf[:], "w3")
         e = keep.tile([P, S], F32, name="e")
         h = keep.tile([P, S], F32, name="h")
         for bank, lo, hi in e_banks:
@@ -200,13 +199,11 @@ def tile_picked_edgeatt_sigmoid_p_kernel(tc, x_words, x_scales, w1, w2, w3, offs
             first_pass([bank], w3_q[0])
             second_pass([bank], w3_q[1])
 
-        y_dst0 = keep.tile([P, DST_SPLIT], F32, name="y_dst0", tag="after_w3b_rounding", align_bytes=64)
         y_dst1 = keep.tile([P, U - DST_SPLIT], F32, name="y_dst1", tag="w2b_codes", align_bytes=64)
         logit = keep.tile([P, U], F32, name="logit")
-        gate = keep.tile([P, U], F32, name="gate")
+        gate = keep.tile([P, U], F32, name="gate", tag="w3_codes", align_bytes=64)
         h_src = keep.tile([P, U - SRC_SPLIT], F32, name="h_src")
         result = keep.tile([P, U], F32, name="result")
-        nc.vector.tensor_copy(y_dst0[:], y[:].indirect(entries(dst_sb, 0, DST_SPLIT)))
         for lo, hi in SUM_PIECES[1:]:
             nc.scalar.activation(y_dst1[:, lo - DST_SPLIT : hi - DST_SPLIT], y[:].indirect(entries(dst_sb, lo, hi)), COPY)
         for bank, lo, hi in h_banks:
@@ -216,8 +213,7 @@ def tile_picked_edgeatt_sigmoid_p_kernel(tc, x_words, x_scales, w1, w2, w3, offs
             nc.vector.tensor_tensor(logit[:, lo:hi], e[:].indirect(entries(src_sb, lo, hi)), y_dst, ADD)
         for lo, hi in GATE_PIECES:
             nc.scalar.activation(gate[:, lo:hi], logit[:, lo:hi], SIGMOID)
-        for lo, hi in OUT_PIECES[2:]:
-            nc.scalar.activation(h_src[:, lo - SRC_SPLIT : hi - SRC_SPLIT], h[:].indirect(entries(src_sb, lo, hi)), COPY)
+        nc.scalar.activation(h_src[:], h[:].indirect(entries(src_sb, SRC_SPLIT, U)), COPY)
         for lo, hi in OUT_PIECES:
             if lo < SRC_SPLIT:
                 picked_h = h[:].indirect(entries(src_sb, lo, hi))

@@ -30,10 +30,9 @@ X_SPLIT = 768
 HALVES = [(0, BANK), (BANK, S)]
 PASS_CUTS = [0, 512, X_SPLIT, S]
 DST_SPLIT = 448
-SRC_SPLIT = 704
-SUM_PIECES = [(0, DST_SPLIT), (DST_SPLIT, SRC_SPLIT), (SRC_SPLIT, U)]
-GATE_PIECES = [(0, 320), (320, SRC_SPLIT), (SRC_SPLIT, U)]
-OUT_PIECES = [(0, 320), (320, SRC_SPLIT), (SRC_SPLIT, 896), (896, U)]
+SUM_PIECES = [(0, DST_SPLIT), (DST_SPLIT, 704), (704, U)]
+OUT_PIECES = [(0, 320), (320, 576), (576, 896), (896, U)]
+PLAIN = 2
 
 
 def tile_picked_edgeatt_sigmoid_p_kernel(tc, x_words, x_scales, w1, w2, w3, offs, src, dst, out):
@@ -138,10 +137,10 @@ def tile_picked_edgeatt_sigmoid_p_kernel(tc, x_words, x_scales, w1, w2, w3, offs
         w1a_raw = raw_tile("w1a")
         load_pass(w1a_raw[:], w1, 0)
         table1 = load_words(1)
-        w1b_raw = raw_tile("w1b", tag="after_w1b_rounding")
-        load_pass(w1b_raw[:], w1, 1)
         nc.vector.tensor_copy(sc_picked[:], scale_table[:].indirect(offs_sb[:]))
         place_scales(sc_picked)
+        w1b_raw = raw_tile("w1b", tag="after_w1b_rounding")
+        load_pass(w1b_raw[:], w1, 1)
         w2a_raw = raw_tile("w2a")
         load_pass(w2a_raw[:], w2, 0)
         w2b_raw = raw_tile("w2b")
@@ -202,7 +201,8 @@ def tile_picked_edgeatt_sigmoid_p_kernel(tc, x_words, x_scales, w1, w2, w3, offs
         y_dst1 = keep.tile([P, U - DST_SPLIT], F32, name="y_dst1", tag="w2b_codes", align_bytes=64)
         logit = keep.tile([P, U], F32, name="logit")
         gate = keep.tile([P, U], F32, name="gate", tag="w3_codes", align_bytes=64)
-        h_src = keep.tile([P, U - SRC_SPLIT], F32, name="h_src")
+        plain_lo, plain_hi = OUT_PIECES[PLAIN]
+        h_src = keep.tile([P, plain_hi - plain_lo], F32, name="h_src")
         result = keep.tile([P, U], F32, name="result")
         for lo, hi in SUM_PIECES[1:]:
             nc.scalar.activation(y_dst1[:, lo - DST_SPLIT : hi - DST_SPLIT], y[:].indirect(entries(dst_sb, lo, hi)), COPY)
@@ -211,13 +211,11 @@ def tile_picked_edgeatt_sigmoid_p_kernel(tc, x_words, x_scales, w1, w2, w3, offs
         for lo, hi in SUM_PIECES:
             y_dst = y_dst0[:] if lo < DST_SPLIT else y_dst1[:, lo - DST_SPLIT : hi - DST_SPLIT]
             nc.vector.tensor_tensor(logit[:, lo:hi], e[:].indirect(entries(src_sb, lo, hi)), y_dst, ADD)
-        for lo, hi in GATE_PIECES:
+        for piece, (lo, hi) in enumerate(OUT_PIECES):
+            if piece == PLAIN:
+                nc.scalar.activation(h_src[:], h[:].indirect(entries(src_sb, lo, hi)), COPY)
             nc.scalar.activation(gate[:, lo:hi], logit[:, lo:hi], SIGMOID)
-        nc.scalar.activation(h_src[:], h[:].indirect(entries(src_sb, SRC_SPLIT, U)), COPY)
-        for lo, hi in OUT_PIECES:
-            if lo < SRC_SPLIT:
-                picked_h = h[:].indirect(entries(src_sb, lo, hi))
-            else:
-                picked_h = h_src[:, lo - SRC_SPLIT : hi - SRC_SPLIT]
+        for piece, (lo, hi) in enumerate(OUT_PIECES):
+            picked_h = h_src[:] if piece == PLAIN else h[:].indirect(entries(src_sb, lo, hi))
             nc.vector.tensor_tensor(result[:, lo:hi], picked_h, gate[:, lo:hi], MULT)
             nc.sync.dma_start(out[:, lo:hi], result[:, lo:hi])

@@ -171,7 +171,7 @@ def tile_picked_edgeatt_sigmoid_p_kernel(tc, x_words, x_scales, w1, w2, w3, offs
         w2a_bf = staged("w2a")
         nc.scalar.copy(walk_out(w2a_bf[:, 0]), walk_in(w2a_raw[:]))
         w2b_bf = staged("w2b")
-        nc.vector.tensor_copy(w2b_bf[:, 0], w2b_raw[:].rearrange("p j m -> p m j"))
+        nc.vector.tensor_copy(walk_out(w2b_bf[:, 0]), walk_in(w2b_raw[:]))
         (w2a_q,) = quantize(w2a_bf[:], "w2a")
         (w2b_q,) = quantize(w2b_bf[:], "w2b")
         y = keep.tile([P, S], F32, name="y", align_bytes=64)
@@ -185,7 +185,7 @@ def tile_picked_edgeatt_sigmoid_p_kernel(tc, x_words, x_scales, w1, w2, w3, offs
 
         w3_bf = staged("w3", PASSES)
         for z, raw in enumerate((w3a_raw, w3b_raw)):
-            nc.vector.tensor_copy(w3_bf[:, z], raw[:].rearrange("p j m -> p m j"))
+            nc.vector.tensor_copy(walk_out(w3_bf[:, z]), walk_in(raw[:]))
         y_dst0 = keep.tile([P, DST_SPLIT], F32, name="y_dst0", align_bytes=64)
         nc.vector.tensor_copy(y_dst0[:], y[:].indirect(entries(dst_sb, 0, DST_SPLIT)))
         w3_q = quantize(w3_bf[:], "w3")

@@ -28,10 +28,11 @@ BANK = 512
 
 X_SPLIT = 768
 HALVES = [(0, BANK), (BANK, S)]
+QUARTERS = [(lo, lo + 256) for lo in range(0, S, 256)]
 PASS_CUTS = [0, 512, X_SPLIT, S]
-DST_SPLIT = 448
-SUM_PIECES = [(0, DST_SPLIT), (DST_SPLIT, 704), (704, U)]
-OUT_PIECES = [(0, 320), (320, 576), (576, 896), (896, U)]
+DST_SPLIT = 512
+SUM_PIECES = [(0, 256), (256, DST_SPLIT), (DST_SPLIT, 704), (704, U)]
+OUT_PIECES = [(0, 256), (256, 608), (608, 896), (896, U)]
 PLAIN = 2
 
 
@@ -127,7 +128,7 @@ def tile_picked_edgeatt_sigmoid_p_kernel(tc, x_words, x_scales, w1, w2, w3, offs
 
         def second_pass(group_banks, quantized):
             for bank, first, last in group_banks:
-                cuts = [cut for cut in PASS_CUTS if first <= cut <= last]
+                cuts = [first] + [cut for cut in PASS_CUTS if first < cut < last] + [last]
                 for lo, hi in zip(cuts, cuts[1:]):
                     product(bank[:, lo - first : hi - first], quantized, 1, lo, hi, False, hi == last)
 
@@ -156,7 +157,7 @@ def tile_picked_edgeatt_sigmoid_p_kernel(tc, x_words, x_scales, w1, w2, w3, offs
         w1a_bf = staged("w1a")
         nc.scalar.copy(walk_out(w1a_bf[:, 0]), walk_in(w1a_raw[:]))
         (w1a_q,) = quantize(w1a_bf[:], "w1a")
-        y_banks = banks("y", HALVES, ("bank0", "bank1"))
+        y_banks = banks("y", QUARTERS, ("bank0", "bank1", "bank2", "bank7"))
         first_pass(y_banks, w1a_q)
 
         w1b_bf = staged("w1b")
@@ -187,7 +188,8 @@ def tile_picked_edgeatt_sigmoid_p_kernel(tc, x_words, x_scales, w1, w2, w3, offs
         for z, raw in enumerate((w3a_raw, w3b_raw)):
             nc.vector.tensor_copy(walk_out(w3_bf[:, z]), walk_in(raw[:]))
         y_dst0 = keep.tile([P, DST_SPLIT], F32, name="y_dst0", align_bytes=64)
-        nc.vector.tensor_copy(y_dst0[:], y[:].indirect(entries(dst_sb, 0, DST_SPLIT)))
+        for lo, hi in SUM_PIECES[:2]:
+            nc.vector.tensor_copy(y_dst0[:, lo:hi], y[:].indirect(entries(dst_sb, lo, hi)))
         w3_q = quantize(w3_bf[:], "w3")
         e = keep.tile([P, S], F32, name="e")
         h = keep.tile([P, S], F32, name="h")
@@ -204,12 +206,11 @@ def tile_picked_edgeatt_sigmoid_p_kernel(tc, x_words, x_scales, w1, w2, w3, offs
         plain_lo, plain_hi = OUT_PIECES[PLAIN]
         h_src = keep.tile([P, plain_hi - plain_lo], F32, name="h_src")
         result = keep.tile([P, U], F32, name="result")
-        for lo, hi in SUM_PIECES[1:]:
-            nc.scalar.activation(y_dst1[:, lo - DST_SPLIT : hi - DST_SPLIT], y[:].indirect(entries(dst_sb, lo, hi)), COPY)
+        nc.scalar.activation(y_dst1[:], y[:].indirect(entries(dst_sb, DST_SPLIT, U)), COPY)
         for bank, lo, hi in h_banks:
             nc.scalar.copy(h[:, lo:hi], bank[:])
         for lo, hi in SUM_PIECES:
-            y_dst = y_dst0[:] if lo < DST_SPLIT else y_dst1[:, lo - DST_SPLIT : hi - DST_SPLIT]
+            y_dst = y_dst0[:, lo:hi] if lo < DST_SPLIT else y_dst1[:, lo - DST_SPLIT : hi - DST_SPLIT]
             nc.vector.tensor_tensor(logit[:, lo:hi], e[:].indirect(entries(src_sb, lo, hi)), y_dst, ADD)
         for piece, (lo, hi) in enumerate(OUT_PIECES):
             if piece == PLAIN:

@@ -30,10 +30,11 @@ X_SPLIT = 768
 HALVES = [(0, BANK), (BANK, S)]
 QUARTERS = [(lo, lo + 256) for lo in range(0, S, 256)]
 PASS_CUTS = [0, 512, X_SPLIT, S]
-DST_SPLIT = 512
+DST_SPLIT = 480
 SUM_PIECES = [(0, 256), (256, DST_SPLIT), (DST_SPLIT, 704), (704, U)]
 OUT_PIECES = [(0, 256), (256, 608), (608, 896), (896, U)]
 PLAIN = 2
+W2B_SPLIT = 64
 
 
 def tile_picked_edgeatt_sigmoid_p_kernel(tc, x_words, x_scales, w1, w2, w3, offs, src, dst, out):
@@ -172,14 +173,15 @@ def tile_picked_edgeatt_sigmoid_p_kernel(tc, x_words, x_scales, w1, w2, w3, offs
         w2a_bf = staged("w2a")
         nc.scalar.copy(walk_out(w2a_bf[:, 0]), walk_in(w2a_raw[:]))
         w2b_bf = staged("w2b")
-        nc.vector.tensor_copy(walk_out(w2b_bf[:, 0]), walk_in(w2b_raw[:]))
+        nc.scalar.copy(walk_out(w2b_bf[:, 0, :W2B_SPLIT]), walk_in(w2b_raw[:, :, :W2B_SPLIT]))
+        nc.vector.tensor_copy(walk_out(w2b_bf[:, 0, W2B_SPLIT:]), walk_in(w2b_raw[:, :, W2B_SPLIT:]))
         (w2a_q,) = quantize(w2a_bf[:], "w2a")
         (w2b_q,) = quantize(w2b_bf[:], "w2b")
-        y = keep.tile([P, S], F32, name="y", align_bytes=64)
+        y = keep.tile([P, S], F32, name="y", tag="w2a_raw", align_bytes=64)
         for bank, lo, hi in y_banks:
             nc.scalar.copy(y[:, lo:hi], bank[:])
 
-        e_banks = banks("e", HALVES, ("bank3", "bank4"))
+        e_banks = banks("e", QUARTERS, ("bank3", "bank0", "bank1", "bank2"))
         for bank in e_banks:
             first_pass([bank], w2a_q)
             second_pass([bank], w2b_q)
@@ -195,7 +197,7 @@ def tile_picked_edgeatt_sigmoid_p_kernel(tc, x_words, x_scales, w1, w2, w3, offs
         h = keep.tile([P, S], F32, name="h")
         for bank, lo, hi in e_banks:
             nc.scalar.copy(e[:, lo:hi], bank[:])
-        h_banks = banks("h", HALVES, ("bank5", "bank6"))
+        h_banks = banks("h", HALVES, ("bank4", "bank5"))
         for bank in h_banks:
             first_pass([bank], w3_q[0])
             second_pass([bank], w3_q[1])

@@ -30,11 +30,10 @@ X_SPLIT = 768
 HALVES = [(0, BANK), (BANK, S)]
 QUARTERS = [(lo, lo + 256) for lo in range(0, S, 256)]
 PASS_CUTS = [0, 512, X_SPLIT, S]
-DST_SPLIT = 480
+DST_SPLIT = 512
 SUM_PIECES = [(0, 256), (256, DST_SPLIT), (DST_SPLIT, 704), (704, U)]
 OUT_PIECES = [(0, 256), (256, 608), (608, 896), (896, U)]
 PLAIN = 2
-W2B_SPLIT = 64
 
 
 def tile_picked_edgeatt_sigmoid_p_kernel(tc, x_words, x_scales, w1, w2, w3, offs, src, dst, out):
@@ -173,8 +172,7 @@ def tile_picked_edgeatt_sigmoid_p_kernel(tc, x_words, x_scales, w1, w2, w3, offs
         w2a_bf = staged("w2a")
         nc.scalar.copy(walk_out(w2a_bf[:, 0]), walk_in(w2a_raw[:]))
         w2b_bf = staged("w2b")
-        nc.scalar.copy(walk_out(w2b_bf[:, 0, :W2B_SPLIT]), walk_in(w2b_raw[:, :, :W2B_SPLIT]))
-        nc.vector.tensor_copy(walk_out(w2b_bf[:, 0, W2B_SPLIT:]), walk_in(w2b_raw[:, :, W2B_SPLIT:]))
+        nc.scalar.copy(walk_out(w2b_bf[:, 0]), walk_in(w2b_raw[:]))
         (w2a_q,) = quantize(w2a_bf[:], "w2a")
         (w2b_q,) = quantize(w2b_bf[:], "w2b")
         y = keep.tile([P, S], F32, name="y", tag="w2a_raw", align_bytes=64)

@@ -49,10 +49,10 @@ def tile_picked_edgeatt_sigmoid_p_kernel(tc, x_words, x_scales, w1, w2, w3, offs
         dst_sb = keep.tile([P, U // GROUP], U16, name="dst_sb")
         src_sb = keep.tile([P, U // GROUP], U16, name="src_sb")
 
-        scale_table = keep.tile([P, T], U8, name="scale_table", align_bytes=64)
+        scale_table = keep.tile([P, T], U8, name="scale_table", align_bytes=256)
         nc.vector.memset(scale_table[QUADRANT : 2 * QUADRANT, :].bitcast(I32), 0)
         nc.vector.memset(scale_table[2 * QUADRANT : P, :].bitcast(I32), 0)
-        x_sc = keep.tile([P, S], U8, name="x_sc", align_bytes=64)
+        x_sc = keep.tile([P, S], U8, name="x_sc", align_bytes=256)
         warm_in = keep.tile([P, 1], F32, name="warm_in")
         warm_out = keep.tile([P, 1], F32, name="warm_out")
         nc.gpsimd.memset(warm_in[:], 0.0)
@@ -66,7 +66,7 @@ def tile_picked_edgeatt_sigmoid_p_kernel(tc, x_words, x_scales, w1, w2, w3, offs
                 )
 
         def load_words(z):
-            table = keep.tile([P, T], U32, name=f"word_table{z}", align_bytes=64)
+            table = keep.tile([P, T], U32, name=f"word_table{z}", align_bytes=256)
             nc.sync.dma_start(table[:].bitcast(I32), x_words[z].rearrange("p n t -> p (n t)").bitcast(I32))
             return table
 
@@ -77,7 +77,7 @@ def tile_picked_edgeatt_sigmoid_p_kernel(tc, x_words, x_scales, w1, w2, w3, offs
             )
 
         def raw_tile(name, tag=None):
-            return keep.tile([P, PACK, M], F32, name=name + "_raw", tag=tag or name + "_raw", align_bytes=64)
+            return keep.tile([P, PACK, M], F32, name=name + "_raw", tag=tag or name + "_raw", align_bytes=256)
 
         def walk_out(grouped):
             return grouped.rearrange("p (c i) j -> p c j i", i=2)
@@ -86,19 +86,19 @@ def tile_picked_edgeatt_sigmoid_p_kernel(tc, x_words, x_scales, w1, w2, w3, offs
             return raw.rearrange("p j (c i) -> p c j i", i=2)
 
         def staged(name, passes=1, tag=None):
-            return keep.tile([P, passes, M, PACK], BF16, name=name + "_bf16", tag=tag or name + "_bf16", align_bytes=64)
+            return keep.tile([P, passes, M, PACK], BF16, name=name + "_bf16", tag=tag or name + "_bf16", align_bytes=256)
 
         def quantize(grouped, name):
             passes = grouped.shape[1]
-            codes = keep.tile([P, passes * M], U32, name=name + "_codes", tag=name + "_codes", align_bytes=64)
-            scales = keep.tile([P, passes * M], U8, name=name + "_scales", align_bytes=64)
+            codes = keep.tile([P, passes * M], U32, name=name + "_codes", tag=name + "_codes", align_bytes=256)
+            scales = keep.tile([P, passes * M], U8, name=name + "_scales", align_bytes=256)
             nc.vector.quantize_mx(
                 out=codes[:].bitcast(FP8X4), scales=scales[:], in_=grouped.rearrange("p z m j -> p (z m j)")
             )
             return [(codes[:, z * M : (z + 1) * M], scales[:, z * M : (z + 1) * M]) for z in range(passes)]
 
-        sc_picked = keep.tile([P, S], U8, name="sc_picked", align_bytes=64)
-        x0 = keep.tile([P, S], U32, name="x0", align_bytes=64)
+        sc_picked = keep.tile([P, S], U8, name="sc_picked", align_bytes=256)
+        x0 = keep.tile([P, S], U32, name="x0", align_bytes=256)
         x1_pieces = {}
 
         def picked_words(z, lo, hi):
@@ -162,10 +162,10 @@ def tile_picked_edgeatt_sigmoid_p_kernel(tc, x_words, x_scales, w1, w2, w3, offs
 
         w1b_bf = staged("w1b")
         nc.scalar.copy(walk_out(w1b_bf[:, 0]), walk_in(w1b_raw[:]))
-        x1_pieces[0] = keep.tile([P, X_SPLIT], U32, name="x1_lo", align_bytes=64)
+        x1_pieces[0] = keep.tile([P, X_SPLIT], U32, name="x1_lo", align_bytes=256)
         nc.vector.tensor_copy(x1_pieces[0][:], table1[:].indirect(entries(offs_sb, 0, X_SPLIT)))
         (w1b_q,) = quantize(w1b_bf[:], "w1b")
-        x1_pieces[X_SPLIT] = keep.tile([P, S - X_SPLIT], U32, name="x1_hi", tag="after_w1b_rounding", align_bytes=64)
+        x1_pieces[X_SPLIT] = keep.tile([P, S - X_SPLIT], U32, name="x1_hi", tag="after_w1b_rounding", align_bytes=256)
         nc.vector.tensor_copy(x1_pieces[X_SPLIT][:], table1[:].indirect(entries(offs_sb, X_SPLIT, S)))
         second_pass(y_banks, w1b_q)
 
@@ -175,7 +175,7 @@ def tile_picked_edgeatt_sigmoid_p_kernel(tc, x_words, x_scales, w1, w2, w3, offs
         nc.scalar.copy(walk_out(w2b_bf[:, 0]), walk_in(w2b_raw[:]))
         (w2a_q,) = quantize(w2a_bf[:], "w2a")
         (w2b_q,) = quantize(w2b_bf[:], "w2b")
-        y = keep.tile([P, S], F32, name="y", tag="w2a_raw", align_bytes=64)
+        y = keep.tile([P, S], F32, name="y", tag="w2a_raw", align_bytes=256)
         for bank, lo, hi in y_banks:
             nc.scalar.copy(y[:, lo:hi], bank[:])
 
@@ -184,13 +184,14 @@ def tile_picked_edgeatt_sigmoid_p_kernel(tc, x_words, x_scales, w1, w2, w3, offs
             first_pass([bank], w2a_q)
             second_pass([bank], w2b_q)
 
-        w3_bf = staged("w3", PASSES)
-        for z, raw in enumerate((w3a_raw, w3b_raw)):
-            nc.vector.tensor_copy(walk_out(w3_bf[:, z]), walk_in(raw[:]))
-        y_dst0 = keep.tile([P, DST_SPLIT], F32, name="y_dst0", align_bytes=64)
+        w3a_bf = staged("w3a")
+        nc.vector.tensor_copy(walk_out(w3a_bf[:, 0]), walk_in(w3a_raw[:]))
+        w3b_bf = staged("w3b")
+        nc.vector.tensor_copy(walk_out(w3b_bf[:, 0]), walk_in(w3b_raw[:]))
+        w3_q = quantize(w3a_bf[:], "w3a") + quantize(w3b_bf[:], "w3b")
+        y_dst0 = keep.tile([P, DST_SPLIT], F32, name="y_dst0", align_bytes=256)
         for lo, hi in SUM_PIECES[:2]:
             nc.vector.tensor_copy(y_dst0[:, lo:hi], y[:].indirect(entries(dst_sb, lo, hi)))
-        w3_q = quantize(w3_bf[:], "w3")
         e = keep.tile([P, S], F32, name="e")
         h = keep.tile([P, S], F32, name="h")
         for bank, lo, hi in e_banks:
@@ -200,12 +201,12 @@ def tile_picked_edgeatt_sigmoid_p_kernel(tc, x_words, x_scales, w1, w2, w3, offs
             first_pass([bank], w3_q[0])
             second_pass([bank], w3_q[1])
 
-        y_dst1 = keep.tile([P, U - DST_SPLIT], F32, name="y_dst1", tag="w2b_codes", align_bytes=64)
+        y_dst1 = keep.tile([P, U - DST_SPLIT], F32, name="y_dst1", tag="w2b_codes", align_bytes=256)
         logit = keep.tile([P, U], F32, name="logit")
-        gate = keep.tile([P, U], F32, name="gate", tag="w3_codes", align_bytes=64)
+        gate = keep.tile([P, U], F32, name="gate", tag="w3b_codes", align_bytes=256)
         plain_lo, plain_hi = OUT_PIECES[PLAIN]
         h_src = keep.tile([P, plain_hi - plain_lo], F32, name="h_src")
-        result = keep.tile([P, U], F32, name="result")
+        result = keep.tile([P, U], F32, name="result", align_bytes=256)
         nc.scalar.activation(y_dst1[:], y[:].indirect(entries(dst_sb, DST_SPLIT, U)), COPY)
         for bank, lo, hi in h_banks:
             nc.scalar.copy(h[:, lo:hi], bank[:])

@@ -184,7 +184,7 @@ def tile_picked_edgeatt_sigmoid_p_kernel(tc, x_words, x_scales, w1, w2, w3, offs
             first_pass([bank], w2a_q)
             second_pass([bank], w2b_q)
 
-        w3a_bf = staged("w3a")
+        w3a_bf = staged("w3a", tag="w2b_raw")
         nc.vector.tensor_copy(walk_out(w3a_bf[:, 0]), walk_in(w3a_raw[:]))
         w3b_bf = staged("w3b")
         nc.vector.tensor_copy(walk_out(w3b_bf[:, 0]), walk_in(w3b_raw[:]))

@@ -26,10 +26,11 @@ QUADRANT = 32
 SCALE_ROWS = 4
 BANK = 512
 
-X_SPLIT = 768
+X_SPLIT = 640
+X_LAST = 896
 HALVES = [(0, BANK), (BANK, S)]
 QUARTERS = [(lo, lo + 256) for lo in range(0, S, 256)]
-PASS_CUTS = [0, 512, X_SPLIT, S]
+PASS_CUTS = [0, 512, X_SPLIT, 768, S]
 DST_SPLIT = 512
 SUM_PIECES = [(0, 256), (256, DST_SPLIT), (DST_SPLIT, 704), (704, U)]
 OUT_PIECES = [(0, 256), (256, 608), (608, 896), (896, U)]
@@ -126,9 +127,9 @@ def tile_picked_edgeatt_sigmoid_p_kernel(tc, x_words, x_scales, w1, w2, w3, offs
             for bank, lo, hi in group_banks:
                 product(bank[:], quantized, 0, lo, hi, True, False)
 
-        def second_pass(group_banks, quantized):
+        def second_pass(group_banks, quantized, more_cuts=()):
             for bank, first, last in group_banks:
-                cuts = [first] + [cut for cut in PASS_CUTS if first < cut < last] + [last]
+                cuts = [first] + [cut for cut in sorted(PASS_CUTS + list(more_cuts)) if first < cut < last] + [last]
                 for lo, hi in zip(cuts, cuts[1:]):
                     product(bank[:, lo - first : hi - first], quantized, 1, lo, hi, False, hi == last)
 
@@ -166,8 +167,9 @@ def tile_picked_edgeatt_sigmoid_p_kernel(tc, x_words, x_scales, w1, w2, w3, offs
         nc.vector.tensor_copy(x1_pieces[0][:], table1[:].indirect(entries(offs_sb, 0, X_SPLIT)))
         (w1b_q,) = quantize(w1b_bf[:], "w1b")
         x1_pieces[X_SPLIT] = keep.tile([P, S - X_SPLIT], U32, name="x1_hi", tag="after_w1b_rounding", align_bytes=256)
-        nc.vector.tensor_copy(x1_pieces[X_SPLIT][:], table1[:].indirect(entries(offs_sb, X_SPLIT, S)))
-        second_pass(y_banks, w1b_q)
+        for lo, hi in ((X_SPLIT, X_LAST), (X_LAST, S)):
+            nc.vector.tensor_copy(picked_words(1, lo, hi), table1[:].indirect(entries(offs_sb, lo, hi)))
+        second_pass(y_banks, w1b_q, (X_LAST,))
 
         w2a_bf = staged("w2a")
         nc.scalar.copy(walk_out(w2a_bf[:, 0]), walk_in(w2a_raw[:]))

from contextlib import ExitStack

import concourse.mybir as mybir

K, T, S, M, U = 1024, 2048, 1024, 128, 1024
FLOPS = 3 * 2 * K * M * S

F32 = mybir.dt.float32
BF16 = mybir.dt.bfloat16
I32 = mybir.dt.int32
U32 = mybir.dt.uint32
U16 = mybir.dt.uint16
U8 = mybir.dt.uint8
FP8X4 = mybir.dt.float8_e4m3fn_x4
ADD = mybir.AluOpType.add
MULT = mybir.AluOpType.mult
SIGMOID = mybir.ActivationFunctionType.Sigmoid
COPY = mybir.ActivationFunctionType.Copy

P = 128
PACK = 4
K_PASS = P * PACK
PASSES = K // K_PASS
GROUP = 16
QUADRANT = 32
SCALE_ROWS = 4
BANK = 512

X_SPLIT = 640
X_LAST = 896
HALVES = [(0, BANK), (BANK, S)]
QUARTERS = [(lo, lo + 256) for lo in range(0, S, 256)]
PASS_CUTS = [0, 512, X_SPLIT, 768, S]
DST_SPLIT = 512
SUM_PIECES = [(0, 256), (256, DST_SPLIT), (DST_SPLIT, 704), (704, U)]
OUT_PIECES = [(0, 256), (256, 608), (608, 896), (896, U)]
PLAIN = 2


def tile_picked_edgeatt_sigmoid_p_kernel(tc, x_words, x_scales, w1, w2, w3, offs, src, dst, out):
    nc = tc.nc
    with ExitStack() as ctx:
        keep = ctx.enter_context(tc.tile_pool(name="keep", bufs=1))
        psum = ctx.enter_context(tc.psum_pool(name="psum", bufs=1))

        def entries(list_tile, lo, hi):
            return list_tile[:, lo // GROUP : hi // GROUP]

        offs_sb = keep.tile([P, S // GROUP], U16, name="offs_sb")
        dst_sb = keep.tile([P, U // GROUP], U16, name="dst_sb")
        src_sb = keep.tile([P, U // GROUP], U16, name="src_sb")

        scale_table = keep.tile([P, T], U8, name="scale_table", align_bytes=256)
        nc.vector.memset(scale_table[QUADRANT : 2 * QUADRANT, :].bitcast(I32), 0)
        nc.vector.memset(scale_table[2 * QUADRANT : P, :].bitcast(I32), 0)
        x_sc = keep.tile([P, S], U8, name="x_sc", align_bytes=256)
        warm_in = keep.tile([P, 1], F32, name="warm_in")
        warm_out = keep.tile([P, 1], F32, name="warm_out")
        nc.gpsimd.memset(warm_in[:], 0.0)
        nc.scalar.activation(warm_out[:], warm_in[:], SIGMOID)

        def place_scales(picked):
            for r in range(SCALE_ROWS):
                nc.sync.dma_start(
                    x_sc[r:P:SCALE_ROWS, :].bitcast(I32),
                    picked[PASSES * r : PASSES * r + QUADRANT, :].bitcast(I32),
                )

        def load_words(z):
            table = keep.tile([P, T], U32, name=f"word_table{z}", align_bytes=256)
            nc.sync.dma_start(table[:].bitcast(I32), x_words[z].rearrange("p n t -> p (n t)").bitcast(I32))
            return table

        def load_pass(raw, w, z):
            nc.sync.dma_start(
                raw.rearrange("p j m -> p (j m)"),
                w[z * K_PASS : (z + 1) * K_PASS, :].rearrange("(p j) m -> p (j m)", j=PACK),
            )

        def raw_tile(name, tag=None):
            return keep.tile([P, PACK, M], F32, name=name + "_raw", tag=tag or name + "_raw", align_bytes=256)

        def walk_out(grouped):
            return grouped.rearrange("p (c i) j -> p c j i", i=2)

        def walk_in(raw):
            return raw.rearrange("p j (c i) -> p c j i", i=2)

        def staged(name, passes=1, tag=None):
            return keep.tile([P, passes, M, PACK], BF16, name=name + "_bf16", tag=tag or name + "_bf16", align_bytes=256)

        def quantize(grouped, name):
            passes = grouped.shape[1]
            codes = keep.tile([P, passes * M], U32, name=name + "_codes", tag=name + "_codes", align_bytes=256)
            scales = keep.tile([P, passes * M], U8, name=name + "_scales", align_bytes=256)
            nc.vector.quantize_mx(
                out=codes[:].bitcast(FP8X4), scales=scales[:], in_=grouped.rearrange("p z m j -> p (z m j)")
            )
            return [(codes[:, z * M : (z + 1) * M], scales[:, z * M : (z + 1) * M]) for z in range(passes)]

        sc_picked = keep.tile([P, S], U8, name="sc_picked", align_bytes=256)
        x0 = keep.tile([P, S], U32, name="x0", align_bytes=256)
        x1_pieces = {}

        def picked_words(z, lo, hi):
            if z == 0:
                return x0[:, lo:hi]
            first = 0 if lo < X_SPLIT else X_SPLIT
            return x1_pieces[first][:, lo - first : hi - first]

        def product(bank, quantized, z, lo, hi, start, stop):
            codes, scales = quantized
            nc.tensor.matmul_mx(
                out=bank,
                lhsT=codes.bitcast(FP8X4),
                lhsT_scale=scales,
                rhs=picked_words(z, lo, hi).bitcast(FP8X4),
                rhs_scale=x_sc[SCALE_ROWS * z : P, lo:hi],
                start=start,
                stop=stop,
            )

        def banks(name, groups, tags):
            return [(psum.tile([P, hi - lo], F32, name=f"{name}_bank{lo}", tag=tag), lo, hi) for (lo, hi), tag in zip(groups, tags)]

        def first_pass(group_banks, quantized):
            for bank, lo, hi in group_banks:
                product(bank[:], quantized, 0, lo, hi, True, False)

        def second_pass(group_banks, quantized, more_cuts=()):
            for bank, first, last in group_banks:
                cuts = [first] + [cut for cut in sorted(PASS_CUTS + list(more_cuts)) if first < cut < last] + [last]
                for lo, hi in zip(cuts, cuts[1:]):
                    product(bank[:, lo - first : hi - first], quantized, 1, lo, hi, False, hi == last)

        nc.sync.dma_start(scale_table[0:QUADRANT, :].bitcast(I32), x_scales.rearrange("z r c -> r z c").bitcast(I32))
        nc.sync.dma_start(offs_sb[:], offs)
        table0 = load_words(0)
        w1a_raw = raw_tile("w1a")
        load_pass(w1a_raw[:], w1, 0)
        table1 = load_words(1)
        nc.vector.tensor_copy(sc_picked[:], scale_table[:].indirect(offs_sb[:]))
        place_scales(sc_picked)
        w1b_raw = raw_tile("w1b", tag="after_w1b_rounding")
        load_pass(w1b_raw[:], w1, 1)
        w2a_raw = raw_tile("w2a")
        load_pass(w2a_raw[:], w2, 0)
        w2b_raw = raw_tile("w2b")
        load_pass(w2b_raw[:], w2, 1)
        w3a_raw = raw_tile("w3a")
        load_pass(w3a_raw[:], w3, 0)
        w3b_raw = raw_tile("w3b")
        load_pass(w3b_raw[:], w3, 1)
        nc.sync.dma_start(dst_sb[:], dst)
        nc.sync.dma_start(src_sb[:], src)

        nc.vector.tensor_copy(x0[:], table0[:].indirect(offs_sb[:]))
        w1a_bf = staged("w1a")
        nc.scalar.copy(walk_out(w1a_bf[:, 0]), walk_in(w1a_raw[:]))
        (w1a_q,) = quantize(w1a_bf[:], "w1a")
        y_banks = banks("y", QUARTERS, ("bank0", "bank1", "bank2", "bank7"))
        first_pass(y_banks, w1a_q)

        w1b_bf = staged("w1b")
        nc.scalar.copy(walk_out(w1b_bf[:, 0]), walk_in(w1b_raw[:]))
        x1_pieces[0] = keep.tile([P, X_SPLIT], U32, name="x1_lo", align_bytes=256)
        nc.vector.tensor_copy(x1_pieces[0][:], table1[:].indirect(entries(offs_sb, 0, X_SPLIT)))
        (w1b_q,) = quantize(w1b_bf[:], "w1b")
        x1_pieces[X_SPLIT] = keep.tile([P, S - X_SPLIT], U32, name="x1_hi", tag="after_w1b_rounding", align_bytes=256)
        for lo, hi in ((X_SPLIT, X_LAST), (X_LAST, S)):
            nc.vector.tensor_copy(picked_words(1, lo, hi), table1[:].indirect(entries(offs_sb, lo, hi)))
        second_pass(y_banks, w1b_q, (X_LAST,))

        w2a_bf = staged("w2a")
        nc.scalar.copy(walk_out(w2a_bf[:, 0]), walk_in(w2a_raw[:]))
        w2b_bf = staged("w2b")
        nc.scalar.copy(walk_out(w2b_bf[:, 0]), walk_in(w2b_raw[:]))
        (w2a_q,) = quantize(w2a_bf[:], "w2a")
        (w2b_q,) = quantize(w2b_bf[:], "w2b")
        y = keep.tile([P, S], F32, name="y", tag="w2a_raw", align_bytes=256)
        for bank, lo, hi in y_banks:
            nc.scalar.copy(y[:, lo:hi], bank[:])

        e_banks = banks("e", QUARTERS, ("bank3", "bank0", "bank1", "bank2"))
        for bank in e_banks:
            first_pass([bank], w2a_q)
            second_pass([bank], w2b_q)

        w3a_bf = staged("w3a", tag="w2b_raw")
        nc.vector.tensor_copy(walk_out(w3a_bf[:, 0]), walk_in(w3a_raw[:]))
        w3b_bf = staged("w3b")
        nc.vector.tensor_copy(walk_out(w3b_bf[:, 0]), walk_in(w3b_raw[:]))
        w3_q = quantize(w3a_bf[:], "w3a") + quantize(w3b_bf[:], "w3b")
        y_dst0 = keep.tile([P, DST_SPLIT], F32, name="y_dst0", align_bytes=256)
        for lo, hi in SUM_PIECES[:2]:
            nc.vector.tensor_copy(y_dst0[:, lo:hi], y[:].indirect(entries(dst_sb, lo, hi)))
        e = keep.tile([P, S], F32, name="e")
        h = keep.tile([P, S], F32, name="h")
        for bank, lo, hi in e_banks:
            nc.scalar.copy(e[:, lo:hi], bank[:])
        h_banks = banks("h", HALVES, ("bank4", "bank5"))
        for bank in h_banks:
            first_pass([bank], w3_q[0])
            second_pass([bank], w3_q[1])

        y_dst1 = keep.tile([P, U - DST_SPLIT], F32, name="y_dst1", tag="w2b_codes", align_bytes=256)
        logit = keep.tile([P, U], F32, name="logit")
        gate = keep.tile([P, U], F32, name="gate", tag="w3b_codes", align_bytes=256)
        plain_lo, plain_hi = OUT_PIECES[PLAIN]
        h_src = keep.tile([P, plain_hi - plain_lo], F32, name="h_src")
        result = keep.tile([P, U], F32, name="result", align_bytes=256)
        nc.scalar.activation(y_dst1[:], y[:].indirect(entries(dst_sb, DST_SPLIT, U)), COPY)
        for bank, lo, hi in h_banks:
            nc.scalar.copy(h[:, lo:hi], bank[:])
        for lo, hi in SUM_PIECES:
            y_dst = y_dst0[:, lo:hi] if lo < DST_SPLIT else y_dst1[:, lo - DST_SPLIT : hi - DST_SPLIT]
            nc.vector.tensor_tensor(logit[:, lo:hi], e[:].indirect(entries(src_sb, lo, hi)), y_dst, ADD)
        for piece, (lo, hi) in enumerate(OUT_PIECES):
            if piece == PLAIN:
                nc.scalar.activation(h_src[:], h[:].indirect(entries(src_sb, lo, hi)), COPY)
            nc.scalar.activation(gate[:, lo:hi], logit[:, lo:hi], SIGMOID)
        for piece, (lo, hi) in enumerate(OUT_PIECES):
            picked_h = h_src[:] if piece == PLAIN else h[:].indirect(entries(src_sb, lo, hi))
            nc.vector.tensor_tensor(result[:, lo:hi], picked_h, gate[:, lo:hi], MULT)
            nc.sync.dma_start(out[:, lo:hi], result[:, lo:hi])
